import numpy as np
import ml_dtypes


def mxq(x, axis, fmt="e4m3"):
    dtype, down = {"e4m3": (ml_dtypes.float8_e4m3fn, 7), "e5m2": (ml_dtypes.float8_e5m2, 14)}[fmt]
    v = np.moveaxis(np.asarray(x, np.float32).astype(ml_dtypes.bfloat16).astype(np.float64), axis, -1)
    blocks = v.reshape(v.shape[:-1] + (-1, 32))
    amax = np.abs(blocks).max(-1, keepdims=True)
    byte = np.maximum(np.where(amax > 0, np.frexp(amax)[1] - 1 + 127, 0) - down, 1)
    scale = np.exp2(byte - 127.0)
    codes = (blocks / scale).astype(np.float32).astype(dtype).astype(np.float64)
    return np.moveaxis((codes * scale).reshape(v.shape), -1, axis)


WIDE = False


def mx_kscale(k):
    if not WIDE:
        return np.ones(k)
    levels = np.array([24, -24, 12, -12, 0])
    if k % 512:
        return np.exp2(np.random.permutation(np.resize(levels, k // 32))).repeat(32)
    a = np.empty((k // 512, 16))
    for p in range(k // 512):
        a[p, :8] = np.random.permutation(np.resize(levels, 8))
        for g in range(8):
            far = levels[np.abs(levels - a[p, g]) >= 10]
            a[p, g + 8] = far[np.random.randint(len(far))]
    return np.exp2(a.ravel()).repeat(32)


def f64(x):
    return np.asarray(x).astype(np.float64)


def striped(idx):
    return np.tile(idx.reshape(-1, 16).T, (8, 1)).astype(np.uint16)


def unstriped(offs):
    return offs[:16].T.reshape(-1).astype(np.int64)


E2M1 = np.array([0.0, 0.5, 1.0, 1.5, 2.0, 3.0, 4.0, 6.0, -0.0, -0.5, -1.0, -1.5, -2.0, -3.0, -4.0, -6.0])


def pack_weight(w, fmt):
    k, n = w.shape
    w = f64(np.asarray(w, np.float32).astype(ml_dtypes.bfloat16)).reshape(k // 32, 32, n)
    amax = np.abs(w).max(1)
    if fmt == "e4m3":
        byte = np.frexp(amax)[1] - 1 + 127 - 7
    else:
        mant, ex = np.frexp(amax / 6.0)
        byte = np.where(mant > 0.5, ex, ex - 1) + 127
    byte = np.clip(np.where(amax > 0, byte, 1), 1, 254)
    scaled = (w * np.exp2(127.0 - byte)[:, None, :]).reshape(k, n).astype(np.float32)
    by_word = np.ascontiguousarray(scaled.reshape(k // 512, 128, 4, n).transpose(0, 1, 3, 2))
    if fmt == "e4m3":
        words = by_word.astype(ml_dtypes.float8_e4m3fn).view(np.uint8)
    else:
        c = by_word.astype(ml_dtypes.float4_e2m1fn).view(np.uint8) & 0xF
        words = (c[..., 0::2] | (c[..., 1::2] << 4)).reshape(k // 512, 128, 2 * n)
    return np.ascontiguousarray(words), np.ascontiguousarray(byte.astype(np.uint8).reshape(k // 512, 16, n))


def unpack_weight(words, scales, fmt):
    g, _, n = scales.shape
    words = np.ascontiguousarray(words).reshape(g, 128, n, -1)
    if fmt == "e4m3":
        vals = words.view(ml_dtypes.float8_e4m3fn).astype(np.float64)
    else:
        nib = np.empty((g, 128, n, 4), np.uint8)
        nib[..., 0::2] = words & 0xF
        nib[..., 1::2] = words >> 4
        vals = E2M1[nib]
    vals = vals * np.repeat(np.exp2(scales.astype(np.float64) - 127.0), 8, axis=1)[..., None]
    return vals.transpose(0, 1, 3, 2).reshape(g * 512, n)


K, R, N, T, J = 512, 512, 512, 4096, 512


def setup_inputs():
    n = np.random.standard_normal
    s = mx_kscale(K)[:, None]
    u = mx_kscale(R)[:, None]
    p_tab = pack_weight(n((K, T)) * s, "e4m3")
    p_w = pack_weight(n((K, R)) / np.sqrt(K) / s * u.T, "e2m1")
    p_wd = pack_weight(n((R, N)) / np.sqrt(R) / u, "e2m1")
    return {
        "tab_words": p_tab[0],
        "tab_scales": p_tab[1],
        "c": (n((K, J)) * s).astype(np.float32),
        "w_words": p_w[0],
        "w_scales": p_w[1],
        "wc": (n((K, R)) / np.sqrt(K) / s * u.T).astype(np.float32),
        "wd_words": p_wd[0],
        "wd_scales": p_wd[1],
        "gm": (n((N, J))).astype(np.float32),
        "offs": striped(np.concatenate([np.random.permutation(T)[:J] for _ in range(3)])),
    }


def reference(tab_words, tab_scales, c, w_words, w_scales, wc, wd_words, wd_scales, gm, offs):
    idx = unstriped(offs).reshape(3, J)
    tab_ = unpack_weight(tab_words, tab_scales, "e4m3")[:, idx]
    c_ = mxq(f64(c), 0, "e4m3")
    w_ = unpack_weight(w_words, w_scales, "e2m1")
    a0 = w_.T @ tab_[:, 0]
    a1 = w_.T @ tab_[:, 1]
    a2 = w_.T @ tab_[:, 2]
    wc_ = mxq(f64(wc), 0, "e4m3")
    ac = wc_.T @ c_
    h = np.maximum(np.maximum(np.maximum(a0, a1), a2) + ac, 0.0)
    h_ = mxq(h, 0, "e4m3")
    wd_ = unpack_weight(wd_words, wd_scales, "e2m1")
    y = wd_.T @ h_
    return y * f64(gm)

@@ -1,0 +1,177 @@
+from contextlib import ExitStack
+
+import concourse.mybir as mybir
+
+K, R, N, T, J = 512, 512, 512, 4096, 512
+G = 3
+FLOPS = 2 * K * R * J * (G + 1) + 2 * R * N * J
+
+F32 = mybir.dt.float32
+BF16 = mybir.dt.bfloat16
+I32 = mybir.dt.int32
+U32 = mybir.dt.uint32
+U16 = mybir.dt.uint16
+U8 = mybir.dt.uint8
+FP8X4 = mybir.dt.float8_e4m3fn_x4
+FP4X4 = mybir.dt.float4_e2m1fn_x4
+ALU = mybir.AluOpType
+ACT = mybir.ActivationFunctionType
+
+P = 128
+PACK = 4
+CH = 128
+NCH = J // CH
+HALF = 256
+
+
+def load_scale_rows(queue, plane, rows):
+    for q in range(4):
+        queue.dma_start(out=plane[32 * q : 32 * q + 4, :].bitcast(I32), in_=rows[4 * q : 4 * q + 4, :].bitcast(I32))
+
+
+def tile_list_pnet_gate_kernel(
+    tc, tab_words, tab_scales, c, w_words, w_scales, wc, wd_words, wd_scales, gm, offs, out
+):
+    nc = tc.nc
+    with ExitStack() as ctx:
+        keep = ctx.enter_context(tc.tile_pool(name="keep", bufs=1))
+        psum = ctx.enter_context(tc.psum_pool(name="psum", bufs=8))
+
+        def sb(name, shape, dtype, tag=None):
+            return keep.tile(shape, dtype, name=name, tag=tag or name, align_bytes=64)
+
+        offsets = keep.tile([P, G * J // 16], U16, name="offsets")
+        nc.sync.dma_start(offsets[:], offs)
+
+        tab_s = sb("tab_s", [P, T], U8)
+        w_s_raw = sb("w_s_raw", [P, R], U8)
+        nc.vector.memset(tab_s[:].bitcast(I32), 0)
+        nc.gpsimd.memset(w_s_raw[:].bitcast(I32), 0)
+        load_scale_rows(nc.gpsimd, w_s_raw, w_scales[0])
+
+        def load_c(hf, tag):
+            raw = sb("c_raw%d" % hf, [P, PACK, HALF], F32, tag)
+            nc.sync.dma_start(out=raw[:], in_=c[:, hf * HALF : (hf + 1) * HALF].rearrange("(p i) j -> p i j", i=PACK))
+            return raw
+
+        def round_c(hf, raw):
+            rounded = sb("c_bf%d" % hf, [P, HALF * PACK], BF16)
+            nc.scalar.activation(
+                rounded[:].rearrange("p (a b i) -> p a i b", b=4, i=PACK),
+                raw[:].rearrange("p i (a b) -> p a i b", b=4),
+                ACT.Copy,
+            )
+            return rounded
+
+        def quantize(name, rounded, width):
+            words = sb(name + "_w", [P, width], U32)
+            scales = sb(name + "_s", [P, width], U8)
+            nc.vector.quantize_mx(out=words[:].bitcast(FP8X4), scales=scales[:], in_=rounded[:])
+            return words, scales
+
+        w_raw = sb("w_raw", [P, 2 * R], U8)
+        nc.sync.dma_start(out=w_raw[:].bitcast(I32), in_=w_words[0].bitcast(I32))
+        c_raw0 = load_c(0, "c_raw0")
+        load_scale_rows(nc.sync, tab_s, tab_scales[0])
+
+        w_w = sb("w_w", [P, 2 * R], U8)
+        nc.vector.tensor_copy(
+            w_w[:].bitcast(U16).rearrange("p (t m) -> p t m", t=PACK),
+            w_raw[:].bitcast(U16).rearrange("p (m t) -> p t m", t=PACK),
+        )
+        tab_w = sb("tab_w", [P, T], U32, "w_raw")
+        nc.sync.dma_start(out=tab_w[:].bitcast(I32), in_=tab_words[0].rearrange("p t i -> p (t i)").bitcast(I32))
+
+        c_bf0 = round_c(0, c_raw0)
+        wc_raw = sb("wc_raw", [P, PACK, R], F32, "c_raw0")
+        nc.sync.dma_start(out=wc_raw[:], in_=wc.rearrange("(p i) r -> p i r", i=PACK))
+
+        g_s, g_w = [], []
+        for g in range(G):
+            g_s.append(sb("g_s%d" % g, [P, J], U8))
+            nc.vector.tensor_copy(g_s[g][:], tab_s[:].indirect(offsets[:, g * J // 16 : (g + 1) * J // 16]))
+        c_raw1 = load_c(1, "tab_s")
+
+        w_s = sb("w_s", [P, R], U8)
+        nc.vector.tensor_copy(
+            w_s[:].rearrange("p (t m) -> p t m", t=PACK), w_s_raw[:].rearrange("p (m t) -> p t m", t=PACK)
+        )
+        c_q = [quantize("c0", c_bf0, HALF)]
+        wd_w = sb("wd_w", [P, 2 * N], U8, "c_bf0")
+        nc.sync.dma_start(out=wd_w[:].bitcast(I32), in_=wd_words[0].bitcast(I32))
+        wd_s = sb("wd_s", [P, N], U8, "w_s_raw")
+        nc.gpsimd.memset(wd_s[:].bitcast(I32), 0)
+        load_scale_rows(nc.sync, wd_s, wd_scales[0])
+
+        for g in range(G):
+            g_w.append(sb("g_w%d" % g, [P, J], U32))
+            nc.vector.tensor_copy(g_w[g][:], tab_w[:].indirect(offsets[:, g * J // 16 : (g + 1) * J // 16]))
+        gate = sb("gate", [P, N // P, J], F32, "w_raw")
+        nc.sync.dma_start(out=gate[:], in_=gm.rearrange("(u p) j -> p u j", p=P))
+
+        def product(lhs, lhs_bytes, lhs_dtype, lhs_s, rhs, rhs_s):
+            bank = psum.tile([P, PACK, CH], F32, name="bank")
+            for t in range(PACK):
+                nc.tensor.matmul_mx(
+                    out=bank[:, t, :],
+                    lhsT=lhs[:, t * P * lhs_bytes : (t + 1) * P * lhs_bytes].bitcast(lhs_dtype),
+                    lhsT_scale=lhs_s[:, t * P : (t + 1) * P],
+                    rhs=rhs.bitcast(FP8X4),
+                    rhs_scale=rhs_s,
+                    start=True,
+                    stop=True,
+                )
+            return bank
+
+        def neighbour(g, ch):
+            cols = slice(ch * CH, (ch + 1) * CH)
+            return product(w_w, 2, FP4X4, w_s, g_w[g][:, cols], g_s[g][:, cols])
+
+        def woven(bank):
+            return bank[:].rearrange("p t j -> p j t")
+
+        pooled = []
+        a0 = []
+        for ch in range(NCH):
+            bank = neighbour(0, ch)
+            a0.append(sb("a0_%d" % ch, [P, CH, PACK], F32))
+            nc.scalar.activation(a0[ch][:], woven(bank), ACT.Copy)
+
+        wc_bf = sb("wc_bf", [P, R * PACK], BF16)
+        nc.scalar.activation(
+            wc_bf[:].rearrange("p (t m i) -> p m i t", t=PACK, i=PACK),
+            wc_raw[:].rearrange("p i (m t) -> p m i t", t=PACK),
+            ACT.Copy,
+        )
+        c_bf1 = round_c(1, c_raw1)
+
+        m01 = []
+        for ch in range(NCH):
+            bank = neighbour(1, ch)
+            m01.append(sb("m01_%d" % ch, [P, CH, PACK], F32))
+            nc.vector.tensor_tensor(m01[ch][:], woven(bank), a0[ch][:], ALU.max)
+        for ch in range(NCH):
+            bank = neighbour(2, ch)
+            pooled.append(sb("pooled_%d" % ch, [P, CH, PACK], F32))
+            nc.vector.tensor_tensor(pooled[ch][:], woven(bank), m01[ch][:], ALU.max)
+
+        wc_w, wc_s = quantize("wc", wc_bf, R)
+        c_q.append(quantize("c1", c_bf1, HALF))
+
+        h_bf = []
+        for ch in range(NCH):
+            hf, cols = ch * CH // HALF, slice(ch * CH % HALF, ch * CH % HALF + CH)
+            bank = product(wc_w, 1, FP8X4, wc_s, c_q[hf][0][:, cols], c_q[hf][1][:, cols])
+            z = sb("z%d" % ch, [P, CH, PACK], F32)
+            nc.vector.tensor_tensor(z[:], woven(bank), pooled[ch][:], ALU.add)
+            h_bf.append(sb("h_bf%d" % ch, [P, CH * PACK], BF16))
+            nc.scalar.activation(h_bf[ch][:], z[:].rearrange("p j t -> p (j t)"), ACT.Relu)
+
+        for ch in range(NCH):
+            h_w, h_s = quantize("h%d" % ch, h_bf[ch], CH)
+            bank = product(wd_w, 2, FP4X4, wd_s, h_w[:], h_s[:])
+            res = sb("res%d" % ch, [P, N // P, CH], F32)
+            nc.vector.tensor_tensor(res[:], bank[:], gate[:, :, ch * CH : (ch + 1) * CH], ALU.mult)
+            nc.sync.dma_start(
+                out=out[:, ch * CH : (ch + 1) * CH].rearrange("(u p) j -> p u j", p=P), in_=res[:]
+            )

@@ -22,6 +22,7 @@ PACK = 4
 CH = 128
 NCH = J // CH
 HALF = 256
+T_HEAD = 512
 
 
 def load_scale_rows(queue, plane, rows):
@@ -45,21 +46,25 @@ def tile_list_pnet_gate_kernel(
 
         tab_s = sb("tab_s", [P, T], U8)
         w_s_raw = sb("w_s_raw", [P, R], U8)
+        wd_s = sb("wd_s", [P, N], U8)
         nc.vector.memset(tab_s[:].bitcast(I32), 0)
         nc.gpsimd.memset(w_s_raw[:].bitcast(I32), 0)
-        load_scale_rows(nc.gpsimd, w_s_raw, w_scales[0])
+        nc.gpsimd.memset(wd_s[:].bitcast(I32), 0)
 
-        def load_c(hf, tag):
-            raw = sb("c_raw%d" % hf, [P, PACK, HALF], F32, tag)
+        def load_c(hf):
+            raw = sb("c_raw%d" % hf, [P, PACK, HALF], F32)
             nc.sync.dma_start(out=raw[:], in_=c[:, hf * HALF : (hf + 1) * HALF].rearrange("(p i) j -> p i j", i=PACK))
             return raw
 
         def round_c(hf, raw):
             rounded = sb("c_bf%d" % hf, [P, HALF * PACK], BF16)
-            nc.scalar.activation(
-                rounded[:].rearrange("p (a b i) -> p a i b", b=4, i=PACK),
-                raw[:].rearrange("p i (a b) -> p a i b", b=4),
-                ACT.Copy,
+            nc.gpsimd.tensor_scalar(
+                rounded[:].rearrange("p (j i) -> p j i", i=PACK),
+                raw[:].rearrange("p i j -> p j i"),
+                1.0,
+                0.0,
+                ALU.mult,
+                ALU.add,
             )
             return rounded
 
@@ -71,43 +76,38 @@ def tile_list_pnet_gate_kernel(
 
         w_raw = sb("w_raw", [P, 2 * R], U8)
         nc.sync.dma_start(out=w_raw[:].bitcast(I32), in_=w_words[0].bitcast(I32))
-        c_raw0 = load_c(0, "c_raw0")
+        tab_w = sb("tab_w", [P, T], U32)
+        tab_rows = tab_words[0].rearrange("p t i -> p (t i)").bitcast(I32)
+        nc.sync.dma_start(out=tab_w[:, :T_HEAD].bitcast(I32), in_=tab_rows[:, :T_HEAD])
         load_scale_rows(nc.sync, tab_s, tab_scales[0])
+        nc.sync.dma_start(out=tab_w[:, T_HEAD:].bitcast(I32), in_=tab_rows[:, T_HEAD:])
+        load_scale_rows(nc.sync, w_s_raw, w_scales[0])
+        wc_raw = sb("wc_raw", [P, PACK, R], F32)
+        nc.sync.dma_start(out=wc_raw[:], in_=wc.rearrange("(p i) r -> p i r", i=PACK))
+        c_raw = [load_c(hf) for hf in range(J // HALF)]
+        wd_w = sb("wd_w", [P, 2 * N], U8)
+        nc.sync.dma_start(out=wd_w[:].bitcast(I32), in_=wd_words[0].bitcast(I32))
+        load_scale_rows(nc.sync, wd_s, wd_scales[0])
+        gate = sb("gate", [P, N // P, J], F32)
+        nc.sync.dma_start(out=gate[:], in_=gm.rearrange("(u p) j -> p u j", p=P))
 
         w_w = sb("w_w", [P, 2 * R], U8)
         nc.vector.tensor_copy(
             w_w[:].bitcast(U16).rearrange("p (t m) -> p t m", t=PACK),
             w_raw[:].bitcast(U16).rearrange("p (m t) -> p t m", t=PACK),
         )
-        tab_w = sb("tab_w", [P, T], U32, "w_raw")
-        nc.sync.dma_start(out=tab_w[:].bitcast(I32), in_=tab_words[0].rearrange("p t i -> p (t i)").bitcast(I32))
-
-        c_bf0 = round_c(0, c_raw0)
-        wc_raw = sb("wc_raw", [P, PACK, R], F32, "c_raw0")
-        nc.sync.dma_start(out=wc_raw[:], in_=wc.rearrange("(p i) r -> p i r", i=PACK))
+        w_s = sb("w_s", [P, R], U8)
+        nc.gpsimd.tensor_copy(
+            w_s[:].rearrange("p (t m) -> p t m", t=PACK), w_s_raw[:].rearrange("p (m t) -> p t m", t=PACK)
+        )
 
         g_s, g_w = [], []
         for g in range(G):
             g_s.append(sb("g_s%d" % g, [P, J], U8))
             nc.vector.tensor_copy(g_s[g][:], tab_s[:].indirect(offsets[:, g * J // 16 : (g + 1) * J // 16]))
-        c_raw1 = load_c(1, "tab_s")
-
-        w_s = sb("w_s", [P, R], U8)
-        nc.vector.tensor_copy(
-            w_s[:].rearrange("p (t m) -> p t m", t=PACK), w_s_raw[:].rearrange("p (m t) -> p t m", t=PACK)
-        )
-        c_q = [quantize("c0", c_bf0, HALF)]
-        wd_w = sb("wd_w", [P, 2 * N], U8, "c_bf0")
-        nc.sync.dma_start(out=wd_w[:].bitcast(I32), in_=wd_words[0].bitcast(I32))
-        wd_s = sb("wd_s", [P, N], U8, "w_s_raw")
-        nc.gpsimd.memset(wd_s[:].bitcast(I32), 0)
-        load_scale_rows(nc.sync, wd_s, wd_scales[0])
-
         for g in range(G):
             g_w.append(sb("g_w%d" % g, [P, J], U32))
             nc.vector.tensor_copy(g_w[g][:], tab_w[:].indirect(offsets[:, g * J // 16 : (g + 1) * J // 16]))
-        gate = sb("gate", [P, N // P, J], F32, "w_raw")
-        nc.sync.dma_start(out=gate[:], in_=gm.rearrange("(u p) j -> p u j", p=P))
 
         def product(lhs, lhs_bytes, lhs_dtype, lhs_s, rhs, rhs_s):
             bank = psum.tile([P, PACK, CH], F32, name="bank")
@@ -143,20 +143,25 @@ def tile_list_pnet_gate_kernel(
             wc_raw[:].rearrange("p i (m t) -> p m i t", t=PACK),
             ACT.Copy,
         )
-        c_bf1 = round_c(1, c_raw1)
+        c_bf = [round_c(hf, c_raw[hf]) for hf in range(J // HALF)]
 
         m01 = []
         for ch in range(NCH):
             bank = neighbour(1, ch)
             m01.append(sb("m01_%d" % ch, [P, CH, PACK], F32))
             nc.vector.tensor_tensor(m01[ch][:], woven(bank), a0[ch][:], ALU.max)
-        for ch in range(NCH):
+
+        def pool_third(ch, tag=None):
             bank = neighbour(2, ch)
-            pooled.append(sb("pooled_%d" % ch, [P, CH, PACK], F32))
+            pooled.append(sb("pooled_%d" % ch, [P, CH, PACK], F32, tag))
             nc.vector.tensor_tensor(pooled[ch][:], woven(bank), m01[ch][:], ALU.max)
 
+        pool_third(0)
+        pool_third(1)
         wc_w, wc_s = quantize("wc", wc_bf, R)
-        c_q.append(quantize("c1", c_bf1, HALF))
+        c_q = [quantize("c%d" % hf, c_bf[hf], HALF) for hf in range(J // HALF)]
+        pool_third(2, "wc_bf")
+        pool_third(3, "c_bf0")
 
         h_bf = []
         for ch in range(NCH):
@@ -166,8 +171,6 @@ def tile_list_pnet_gate_kernel(
             nc.vector.tensor_tensor(z[:], woven(bank), pooled[ch][:], ALU.add)
             h_bf.append(sb("h_bf%d" % ch, [P, CH * PACK], BF16))
             nc.scalar.activation(h_bf[ch][:], z[:].rearrange("p j t -> p (j t)"), ACT.Relu)
-
-        for ch in range(NCH):
             h_w, h_s = quantize("h%d" % ch, h_bf[ch], CH)
             bank = product(wd_w, 2, FP4X4, wd_s, h_w[:], h_s[:])
             res = sb("res%d" % ch, [P, N // P, CH], F32)

@@ -23,6 +23,7 @@ CH = 128
 NCH = J // CH
 HALF = 256
 T_HEAD = 512
+LAST = NCH - 1
 
 
 def load_scale_rows(queue, plane, rows):
@@ -36,7 +37,8 @@ def tile_list_pnet_gate_kernel(
     nc = tc.nc
     with ExitStack() as ctx:
         keep = ctx.enter_context(tc.tile_pool(name="keep", bufs=1))
-        psum = ctx.enter_context(tc.psum_pool(name="psum", bufs=8))
+        psum_a = ctx.enter_context(tc.psum_pool(name="psum_a", bufs=4))
+        psum_b = ctx.enter_context(tc.psum_pool(name="psum_b", bufs=4))
 
         def sb(name, shape, dtype, tag=None):
             return keep.tile(shape, dtype, name=name, tag=tag or name, align_bytes=64)
@@ -55,18 +57,6 @@ def tile_list_pnet_gate_kernel(
             raw = sb("c_raw%d" % hf, [P, PACK, HALF], F32)
             nc.sync.dma_start(out=raw[:], in_=c[:, hf * HALF : (hf + 1) * HALF].rearrange("(p i) j -> p i j", i=PACK))
             return raw
-
-        def round_c(hf, raw):
-            rounded = sb("c_bf%d" % hf, [P, HALF * PACK], BF16)
-            nc.gpsimd.tensor_scalar(
-                rounded[:].rearrange("p (j i) -> p j i", i=PACK),
-                raw[:].rearrange("p i j -> p j i"),
-                1.0,
-                0.0,
-                ALU.mult,
-                ALU.add,
-            )
-            return rounded
 
         def quantize(name, rounded, width):
             words = sb(name + "_w", [P, width], U32)
@@ -97,45 +87,48 @@ def tile_list_pnet_gate_kernel(
             w_raw[:].bitcast(U16).rearrange("p (m t) -> p t m", t=PACK),
         )
         w_s = sb("w_s", [P, R], U8)
-        nc.gpsimd.tensor_copy(
+        nc.vector.tensor_copy(
             w_s[:].rearrange("p (t m) -> p t m", t=PACK), w_s_raw[:].rearrange("p (m t) -> p t m", t=PACK)
         )
 
-        g_s, g_w = [], []
+        g_s = []
         for g in range(G):
             g_s.append(sb("g_s%d" % g, [P, J], U8))
             nc.vector.tensor_copy(g_s[g][:], tab_s[:].indirect(offsets[:, g * J // 16 : (g + 1) * J // 16]))
+        g_w_first = sb("g_w_first", [P, J], U32)
+        g_w_rest = sb("g_w_rest", [P, (G - 1) * J], U32, "w_s_raw")
+        g_w = [g_w_first[:]] + [g_w_rest[:, g * J : (g + 1) * J] for g in range(G - 1)]
         for g in range(G):
-            g_w.append(sb("g_w%d" % g, [P, J], U32))
-            nc.vector.tensor_copy(g_w[g][:], tab_w[:].indirect(offsets[:, g * J // 16 : (g + 1) * J // 16]))
+            nc.vector.tensor_copy(g_w[g], tab_w[:].indirect(offsets[:, g * J // 16 : (g + 1) * J // 16]))
 
-        def product(lhs, lhs_bytes, lhs_dtype, lhs_s, rhs, rhs_s):
+        def product(psum, *terms):
             bank = psum.tile([P, PACK, CH], F32, name="bank")
             for t in range(PACK):
-                nc.tensor.matmul_mx(
-                    out=bank[:, t, :],
-                    lhsT=lhs[:, t * P * lhs_bytes : (t + 1) * P * lhs_bytes].bitcast(lhs_dtype),
-                    lhsT_scale=lhs_s[:, t * P : (t + 1) * P],
-                    rhs=rhs.bitcast(FP8X4),
-                    rhs_scale=rhs_s,
-                    start=True,
-                    stop=True,
-                )
+                for n, (lhs, lhs_elems, lhs_dtype, lhs_s, rhs, rhs_s) in enumerate(terms):
+                    nc.tensor.matmul_mx(
+                        out=bank[:, t, :],
+                        lhsT=lhs[:, t * P * lhs_elems : (t + 1) * P * lhs_elems].bitcast(lhs_dtype),
+                        lhsT_scale=lhs_s[:, t * P : (t + 1) * P],
+                        rhs=rhs.bitcast(FP8X4),
+                        rhs_scale=rhs_s,
+                        start=n == 0,
+                        stop=n == len(terms) - 1,
+                    )
             return bank
 
         def neighbour(g, ch):
             cols = slice(ch * CH, (ch + 1) * CH)
-            return product(w_w, 2, FP4X4, w_s, g_w[g][:, cols], g_s[g][:, cols])
+            return w_w, 2, FP4X4, w_s, g_w[g][:, cols], g_s[g][:, cols]
 
         def woven(bank):
             return bank[:].rearrange("p t j -> p j t")
 
-        pooled = []
-        a0 = []
-        for ch in range(NCH):
-            bank = neighbour(0, ch)
-            a0.append(sb("a0_%d" % ch, [P, CH, PACK], F32))
-            nc.scalar.activation(a0[ch][:], woven(bank), ACT.Copy)
+        def copy_out(ch, bank):
+            first = sb("first_%d" % ch, [P, CH, PACK], F32)
+            nc.scalar.activation(first[:], woven(bank), ACT.Copy)
+            return first
+
+        firsts = [copy_out(ch, product(psum_a, neighbour(0, ch))) for ch in range(LAST)]
 
         wc_bf = sb("wc_bf", [P, R * PACK], BF16)
         nc.scalar.activation(
@@ -143,38 +136,68 @@ def tile_list_pnet_gate_kernel(
             wc_raw[:].rearrange("p i (m t) -> p m i t", t=PACK),
             ACT.Copy,
         )
-        c_bf = [round_c(hf, c_raw[hf]) for hf in range(J // HALF)]
+        c_bf = [sb("c_bf0", [P, HALF * PACK], BF16, "tab_w"), sb("c_bf1", [P, HALF * PACK], BF16)]
+        nc.gpsimd.tensor_scalar(
+            c_bf[0][:].rearrange("p (j i) -> p j i", i=PACK),
+            c_raw[0][:].rearrange("p i j -> p j i"),
+            1.0,
+            0.0,
+            ALU.mult,
+            ALU.add,
+        )
+        nc.scalar.activation(
+            c_bf[1][:].rearrange("p (a b i) -> p a i b", b=4, i=PACK),
+            c_raw[1][:].rearrange("p i (a b) -> p a i b", b=4),
+            ACT.Copy,
+        )
 
-        m01 = []
-        for ch in range(NCH):
-            bank = neighbour(1, ch)
-            m01.append(sb("m01_%d" % ch, [P, CH, PACK], F32))
-            nc.vector.tensor_tensor(m01[ch][:], woven(bank), a0[ch][:], ALU.max)
+        def running_max(name, bank, so_far, tag=None):
+            larger = sb(name, [P, CH, PACK], F32, tag)
+            nc.vector.tensor_tensor(larger[:], woven(bank), so_far[:], ALU.max)
+            return larger
 
-        def pool_third(ch, tag=None):
-            bank = neighbour(2, ch)
-            pooled.append(sb("pooled_%d" % ch, [P, CH, PACK], F32, tag))
-            nc.vector.tensor_tensor(pooled[ch][:], woven(bank), m01[ch][:], ALU.max)
-
-        pool_third(0)
-        pool_third(1)
+        pairs = [running_max("pair%d" % ch, product(psum_b, neighbour(1, ch)), firsts[ch]) for ch in range(LAST)]
+        c_q = [quantize("c0", c_bf[0], HALF)]
+        pooled = [running_max("pooled0", product(psum_a, neighbour(2, 0)), pairs[0], "tab_w")]
         wc_w, wc_s = quantize("wc", wc_bf, R)
-        c_q = [quantize("c%d" % hf, c_bf[hf], HALF) for hf in range(J // HALF)]
-        pool_third(2, "wc_bf")
-        pool_third(3, "c_bf0")
+        pooled.append(running_max("pooled1", product(psum_a, neighbour(2, 1)), pairs[1], "wc_bf"))
+        c_q.append(quantize("c1", c_bf[1], HALF))
+        pooled.append(running_max("pooled2", product(psum_a, neighbour(2, 2)), pairs[2], "c_bf1"))
 
-        h_bf = []
-        for ch in range(NCH):
+        def own(ch):
             hf, cols = ch * CH // HALF, slice(ch * CH % HALF, ch * CH % HALF + CH)
-            bank = product(wc_w, 1, FP8X4, wc_s, c_q[hf][0][:, cols], c_q[hf][1][:, cols])
+            return wc_w, 1, FP8X4, wc_s, c_q[hf][0][:, cols], c_q[hf][1][:, cols]
+
+        def hidden(ch):
+            bank = product(psum_b, own(ch))
             z = sb("z%d" % ch, [P, CH, PACK], F32)
             nc.vector.tensor_tensor(z[:], woven(bank), pooled[ch][:], ALU.add)
-            h_bf.append(sb("h_bf%d" % ch, [P, CH * PACK], BF16))
-            nc.scalar.activation(h_bf[ch][:], z[:].rearrange("p j t -> p (j t)"), ACT.Relu)
-            h_w, h_s = quantize("h%d" % ch, h_bf[ch], CH)
-            bank = product(wd_w, 2, FP4X4, wd_s, h_w[:], h_s[:])
+            h_bf = sb("h_bf%d" % ch, [P, CH * PACK], BF16)
+            nc.scalar.activation(h_bf[:], z[:].rearrange("p j t -> p (j t)"), ACT.Relu)
+            return h_bf
+
+        def second(ch, h_bf):
+            h_w, h_s = quantize("h%d" % ch, h_bf, CH)
+            return product(psum_a, (wd_w, 2, FP4X4, wd_s, h_w[:], h_s[:]))
+
+        def finish(ch, bank):
+            cols = slice(ch * CH, (ch + 1) * CH)
             res = sb("res%d" % ch, [P, N // P, CH], F32)
-            nc.vector.tensor_tensor(res[:], bank[:], gate[:, :, ch * CH : (ch + 1) * CH], ALU.mult)
-            nc.sync.dma_start(
-                out=out[:, ch * CH : (ch + 1) * CH].rearrange("(u p) j -> p u j", p=P), in_=res[:]
-            )
+            nc.vector.tensor_tensor(res[:], bank[:], gate[:, :, cols], ALU.mult)
+            nc.sync.dma_start(out=out[:, cols].rearrange("(u p) j -> p u j", p=P), in_=res[:])
+
+        h_bf = [hidden(0), hidden(1)]
+        first = copy_out(LAST, product(psum_b, neighbour(0, LAST), own(LAST)))
+        y_banks = [second(0, h_bf[0])]
+        h_bf.append(hidden(2))
+        bank = product(psum_b, neighbour(1, LAST), own(LAST))
+        pair = sb("pair_last", [P, CH, PACK], F32)
+        nc.vector.scalar_tensor_tensor(pair[:], woven(bank), 0.0, first[:], ALU.max, ALU.max)
+        y_banks.append(second(1, h_bf[1]))
+        bank = product(psum_b, neighbour(2, LAST), own(LAST))
+        h_bf.append(sb("h_bf_last", [P, CH * PACK], BF16))
+        nc.vector.tensor_tensor(h_bf[LAST][:].rearrange("p (j t) -> p j t", t=PACK), woven(bank), pair[:], ALU.max)
+        y_banks.append(second(2, h_bf[2]))
+        y_banks.append(second(LAST, h_bf[LAST]))
+        for ch in range(NCH):
+            finish(ch, y_banks[ch])

@@ -27,8 +27,8 @@ LAST = NCH - 1
 
 
 def load_scale_rows(queue, plane, rows):
-    for q in range(4):
-        queue.dma_start(out=plane[32 * q : 32 * q + 4, :].bitcast(I32), in_=rows[4 * q : 4 * q + 4, :].bitcast(I32))
+    for r in range(4):
+        queue.dma_start(out=plane[r:P:32, :].bitcast(I32), in_=rows[r:16:4, :].bitcast(I32))
 
 
 def tile_list_pnet_gate_kernel(
@@ -130,26 +130,19 @@ def tile_list_pnet_gate_kernel(
 
         firsts = [copy_out(ch, product(psum_a, neighbour(0, ch))) for ch in range(LAST)]
 
-        wc_bf = sb("wc_bf", [P, R * PACK], BF16)
-        nc.scalar.activation(
-            wc_bf[:].rearrange("p (t m i) -> p m i t", t=PACK, i=PACK),
-            wc_raw[:].rearrange("p i (m t) -> p m i t", t=PACK),
-            ACT.Copy,
-        )
-        c_bf = [sb("c_bf0", [P, HALF * PACK], BF16, "tab_w"), sb("c_bf1", [P, HALF * PACK], BF16)]
-        nc.gpsimd.tensor_scalar(
-            c_bf[0][:].rearrange("p (j i) -> p j i", i=PACK),
-            c_raw[0][:].rearrange("p i j -> p j i"),
-            1.0,
-            0.0,
-            ALU.mult,
-            ALU.add,
-        )
-        nc.scalar.activation(
-            c_bf[1][:].rearrange("p (a b i) -> p a i b", b=4, i=PACK),
-            c_raw[1][:].rearrange("p i (a b) -> p a i b", b=4),
-            ACT.Copy,
-        )
+        wc_bf = sb("wc_bf", [P, R * PACK], BF16, "tab_w")
+        wc_to = wc_bf[:].rearrange("p (t m i) -> p m t i", t=PACK, i=PACK)
+        wc_from = wc_raw[:].rearrange("p i (m t) -> p m t i", t=PACK)
+        nc.scalar.activation(wc_to[:, :, :2, :], wc_from[:, :, :2, :], ACT.Copy)
+        nc.gpsimd.tensor_scalar(wc_to[:, :, 2:, :], wc_from[:, :, 2:, :], 1.0, 0.0, ALU.mult, ALU.add)
+        c_bf = []
+        for hf in range(J // HALF):
+            c_bf.append(sb("c_bf%d" % hf, [P, HALF * PACK], BF16))
+            nc.scalar.activation(
+                c_bf[hf][:].rearrange("p (a b i) -> p a i b", b=4, i=PACK),
+                c_raw[hf][:].rearrange("p i (a b) -> p a i b", b=4),
+                ACT.Copy,
+            )
 
         def running_max(name, bank, so_far, tag=None):
             larger = sb(name, [P, CH, PACK], F32, tag)
@@ -157,10 +150,10 @@ def tile_list_pnet_gate_kernel(
             return larger
 
         pairs = [running_max("pair%d" % ch, product(psum_b, neighbour(1, ch)), firsts[ch]) for ch in range(LAST)]
-        c_q = [quantize("c0", c_bf[0], HALF)]
-        pooled = [running_max("pooled0", product(psum_a, neighbour(2, 0)), pairs[0], "tab_w")]
+        pooled = [running_max("pooled0", product(psum_a, neighbour(2, 0)), pairs[0])]
         wc_w, wc_s = quantize("wc", wc_bf, R)
-        pooled.append(running_max("pooled1", product(psum_a, neighbour(2, 1)), pairs[1], "wc_bf"))
+        c_q = [quantize("c0", c_bf[0], HALF)]
+        pooled.append(running_max("pooled1", product(psum_a, neighbour(2, 1)), pairs[1], "c_bf0"))
         c_q.append(quantize("c1", c_bf[1], HALF))
         pooled.append(running_max("pooled2", product(psum_a, neighbour(2, 2)), pairs[2], "c_bf1"))
 
@@ -182,9 +175,13 @@ def tile_list_pnet_gate_kernel(
 
         def finish(ch, bank):
             cols = slice(ch * CH, (ch + 1) * CH)
-            res = sb("res%d" % ch, [P, N // P, CH], F32)
-            nc.vector.tensor_tensor(res[:], bank[:], gate[:, :, cols], ALU.mult)
-            nc.sync.dma_start(out=out[:, cols].rearrange("(u p) j -> p u j", p=P), in_=res[:])
+            rows = out[:, cols].rearrange("(u p) j -> p u j", p=P)
+            pieces = 2 if ch == LAST else 1
+            for k in range(pieces):
+                part = slice(k * PACK // pieces, (k + 1) * PACK // pieces)
+                res = sb("res%d_%d" % (ch, k), [P, PACK // pieces, CH], F32)
+                nc.vector.tensor_tensor(res[:], bank[:, part, :], gate[:, part, cols], ALU.mult)
+                nc.sync.dma_start(out=rows[:, part, :], in_=res[:])
 
         h_bf = [hidden(0), hidden(1)]
         first = copy_out(LAST, product(psum_b, neighbour(0, LAST), own(LAST)))

@@ -22,7 +22,6 @@ PACK = 4
 CH = 128
 NCH = J // CH
 HALF = 256
-T_HEAD = 512
 LAST = NCH - 1
 
 
@@ -49,9 +48,11 @@ def tile_list_pnet_gate_kernel(
         tab_s = sb("tab_s", [P, T], U8)
         w_s_raw = sb("w_s_raw", [P, R], U8)
         wd_s = sb("wd_s", [P, N], U8)
+        g_s = sb("g_s", [P, G * J], U8)
         nc.vector.memset(tab_s[:].bitcast(I32), 0)
         nc.gpsimd.memset(w_s_raw[:].bitcast(I32), 0)
-        nc.gpsimd.memset(wd_s[:].bitcast(I32), 0)
+        nc.vector.memset(g_s[:].bitcast(I32), 0)
+        nc.vector.memset(wd_s[:].bitcast(I32), 0)
 
         def load_c(hf):
             raw = sb("c_raw%d" % hf, [P, PACK, HALF], F32)
@@ -66,12 +67,14 @@ def tile_list_pnet_gate_kernel(
 
         w_raw = sb("w_raw", [P, 2 * R], U8)
         nc.sync.dma_start(out=w_raw[:].bitcast(I32), in_=w_words[0].bitcast(I32))
-        tab_w = sb("tab_w", [P, T], U32)
-        tab_rows = tab_words[0].rearrange("p t i -> p (t i)").bitcast(I32)
-        nc.sync.dma_start(out=tab_w[:, :T_HEAD].bitcast(I32), in_=tab_rows[:, :T_HEAD])
-        load_scale_rows(nc.sync, tab_s, tab_scales[0])
-        nc.sync.dma_start(out=tab_w[:, T_HEAD:].bitcast(I32), in_=tab_rows[:, T_HEAD:])
+        nc.sync.dma_start(out=tab_s[0:P:8, :].bitcast(I32), in_=tab_scales[0].bitcast(I32))
         load_scale_rows(nc.sync, w_s_raw, w_scales[0])
+        tab_w = sb("tab_w", [P, T], U32)
+        nc.sync.dma_start(out=tab_w[:].bitcast(I32), in_=tab_words[0].rearrange("p t i -> p (t i)").bitcast(I32))
+        picked_s = sb("picked_s", [P, G * J], U8)
+        nc.vector.tensor_copy(picked_s[:], tab_s[:].indirect(offsets[:]))
+        for r in range(4):
+            nc.sync.dma_start(out=g_s[r:P:32, :].bitcast(I32), in_=picked_s[8 * r : P : 32, :].bitcast(I32))
         wc_raw = sb("wc_raw", [P, PACK, R], F32)
         nc.sync.dma_start(out=wc_raw[:], in_=wc.rearrange("(p i) r -> p i r", i=PACK))
         c_raw = [load_c(hf) for hf in range(J // HALF)]
@@ -91,15 +94,10 @@ def tile_list_pnet_gate_kernel(
             w_s[:].rearrange("p (t m) -> p t m", t=PACK), w_s_raw[:].rearrange("p (m t) -> p t m", t=PACK)
         )
 
-        g_s = []
+        g_w = []
         for g in range(G):
-            g_s.append(sb("g_s%d" % g, [P, J], U8))
-            nc.vector.tensor_copy(g_s[g][:], tab_s[:].indirect(offsets[:, g * J // 16 : (g + 1) * J // 16]))
-        g_w_first = sb("g_w_first", [P, J], U32)
-        g_w_rest = sb("g_w_rest", [P, (G - 1) * J], U32, "w_s_raw")
-        g_w = [g_w_first[:]] + [g_w_rest[:, g * J : (g + 1) * J] for g in range(G - 1)]
-        for g in range(G):
-            nc.vector.tensor_copy(g_w[g], tab_w[:].indirect(offsets[:, g * J // 16 : (g + 1) * J // 16]))
+            g_w.append(sb("g_w%d" % g, [P, J], U32))
+            nc.vector.tensor_copy(g_w[g][:], tab_w[:].indirect(offsets[:, g * J // 16 : (g + 1) * J // 16]))
 
         def product(psum, *terms):
             bank = psum.tile([P, PACK, CH], F32, name="bank")
@@ -118,7 +116,7 @@ def tile_list_pnet_gate_kernel(
 
         def neighbour(g, ch):
             cols = slice(ch * CH, (ch + 1) * CH)
-            return w_w, 2, FP4X4, w_s, g_w[g][:, cols], g_s[g][:, cols]
+            return w_w, 2, FP4X4, w_s, g_w[g][:, cols], g_s[:, g * J + ch * CH : g * J + (ch + 1) * CH]
 
         def woven(bank):
             return bank[:].rearrange("p t j -> p j t")
@@ -191,10 +189,12 @@ def tile_list_pnet_gate_kernel(
         pair = sb("pair_last", [P, CH, PACK], F32)
         nc.vector.scalar_tensor_tensor(pair[:], woven(bank), 0.0, first[:], ALU.max, ALU.max)
         y_banks.append(second(1, h_bf[1]))
+        finish(0, y_banks[0])
         bank = product(psum_b, neighbour(2, LAST), own(LAST))
         h_bf.append(sb("h_bf_last", [P, CH * PACK], BF16))
         nc.vector.tensor_tensor(h_bf[LAST][:].rearrange("p (j t) -> p j t", t=PACK), woven(bank), pair[:], ALU.max)
         y_banks.append(second(2, h_bf[2]))
+        finish(1, y_banks[1])
         y_banks.append(second(LAST, h_bf[LAST]))
-        for ch in range(NCH):
-            finish(ch, y_banks[ch])
+        finish(2, y_banks[2])
+        finish(LAST, y_banks[LAST])

@@ -1,6 +1,7 @@
 from contextlib import ExitStack
 
 import concourse.mybir as mybir
+from concourse.masks import make_identity
 
 K, R, N, T, J = 512, 512, 512, 4096, 512
 G = 3
@@ -23,10 +24,11 @@ CH = 128
 NCH = J // CH
 HALF = 256
 LAST = NCH - 1
+TURNED = 2
 
 
-def load_scale_rows(queue, plane, rows):
-    for r in range(4):
+def load_scale_rows(queue, plane, rows, which=range(4)):
+    for r in which:
         queue.dma_start(out=plane[r:P:32, :].bitcast(I32), in_=rows[r:16:4, :].bitcast(I32))
 
 
@@ -36,8 +38,7 @@ def tile_list_pnet_gate_kernel(
     nc = tc.nc
     with ExitStack() as ctx:
         keep = ctx.enter_context(tc.tile_pool(name="keep", bufs=1))
-        psum_a = ctx.enter_context(tc.psum_pool(name="psum_a", bufs=4))
-        psum_b = ctx.enter_context(tc.psum_pool(name="psum_b", bufs=4))
+        psum = ctx.enter_context(tc.psum_pool(name="psum", bufs=8))
 
         def sb(name, shape, dtype, tag=None):
             return keep.tile(shape, dtype, name=name, tag=tag or name, align_bytes=64)
@@ -53,11 +54,104 @@ def tile_list_pnet_gate_kernel(
         nc.gpsimd.memset(w_s_raw[:].bitcast(I32), 0)
         nc.vector.memset(g_s[:].bitcast(I32), 0)
         nc.vector.memset(wd_s[:].bitcast(I32), 0)
+        load_scale_rows(nc.scalar, w_s_raw, w_scales[0], range(1, 4))
+        ident = sb("ident", [P, P], F32)
+        make_identity(nc, ident[:])
 
-        def load_c(hf):
-            raw = sb("c_raw%d" % hf, [P, PACK, HALF], F32)
-            nc.sync.dma_start(out=raw[:], in_=c[:, hf * HALF : (hf + 1) * HALF].rearrange("(p i) j -> p i j", i=PACK))
+        w_raw = sb("w_raw", [P, 2 * R], U8)
+        nc.sync.dma_start(out=w_raw[:].bitcast(I32), in_=w_words[0].bitcast(I32))
+        load_scale_rows(nc.sync, w_s_raw, w_scales[0], range(1))
+        nc.sync.dma_start(out=tab_s[0:P:8, :].bitcast(I32), in_=tab_scales[0].bitcast(I32))
+        tab_w = sb("tab_w", [P, T], U32)
+        nc.sync.dma_start(out=tab_w[:].bitcast(I32), in_=tab_words[0].rearrange("p t i -> p (t i)").bitcast(I32))
+
+        def load_half(name, matrix, hf):
+            raw = sb(name, [P, PACK, HALF], F32)
+            nc.sync.dma_start(
+                out=raw[:], in_=matrix[:, hf * HALF : (hf + 1) * HALF].rearrange("(p i) j -> p i j", i=PACK)
+            )
             return raw
+
+        wc_raw = [load_half("wc_raw0", wc, 0)]
+        w_w = sb("w_w", [P, 2 * R], U8)
+        nc.vector.tensor_copy(
+            w_w[:].bitcast(U16).rearrange("p (t m) -> p t m", t=PACK),
+            w_raw[:].bitcast(U16).rearrange("p (m t) -> p t m", t=PACK),
+        )
+        picked_s = sb("picked_s", [P, G * J], U8)
+        nc.vector.tensor_copy(picked_s[:], tab_s[:].indirect(offsets[:]))
+        w_s = sb("w_s", [P, R], U8)
+        nc.vector.tensor_copy(
+            w_s[:].rearrange("p (t m) -> p t m", t=PACK), w_s_raw[:].rearrange("p (m t) -> p t m", t=PACK)
+        )
+        for r in range(4):
+            nc.sync.dma_start(out=g_s[r:P:32, :].bitcast(I32), in_=picked_s[8 * r : P : 32, :].bitcast(I32))
+        wc_raw.append(load_half("wc_raw1", wc, 1))
+        c_raw = [load_half("c_raw%d" % hf, c, hf) for hf in range(J // HALF)]
+        wd_w = sb("wd_w", [P, 2 * N], U8)
+        nc.sync.dma_start(out=wd_w[:].bitcast(I32), in_=wd_words[0].bitcast(I32))
+        load_scale_rows(nc.sync, wd_s, wd_scales[0])
+        gate = sb("gate", [P, N // P, J], F32)
+        nc.sync.dma_start(out=gate[:], in_=gm.rearrange("(u p) j -> p u j", p=P))
+
+        g_w = []
+        for g in range(G):
+            g_w.append(sb("g_w%d" % g, [P, J], U32))
+            nc.vector.tensor_copy(g_w[g][:], tab_w[:].indirect(offsets[:, g * J // 16 : (g + 1) * J // 16]))
+
+        def by_point(points, points_s, weight, weight_bytes, weight_dtype, weight_s):
+            bank = psum.tile([P, PACK, P], F32, name="bank")
+            nc.tensor.matmul_mx(
+                out=bank[:].rearrange("p t m -> p (t m)"),
+                lhsT=points.bitcast(FP8X4),
+                lhsT_scale=points_s,
+                rhs=weight[:].bitcast(weight_dtype),
+                rhs_scale=weight_s[:],
+                start=True,
+                stop=True,
+            )
+            return bank
+
+        def by_channel(*terms):
+            bank = psum.tile([P, PACK, CH], F32, name="bank")
+            for t in range(PACK):
+                for n, (points, points_s, weight, elems, weight_dtype, weight_s) in enumerate(terms):
+                    nc.tensor.matmul_mx(
+                        out=bank[:, t, :],
+                        lhsT=weight[:, t * P * elems : (t + 1) * P * elems].bitcast(weight_dtype),
+                        lhsT_scale=weight_s[:, t * P : (t + 1) * P],
+                        rhs=points.bitcast(FP8X4),
+                        rhs_scale=points_s,
+                        start=n == 0,
+                        stop=n == len(terms) - 1,
+                    )
+            return bank
+
+        def project(ch, term):
+            return by_point(*term) if ch < TURNED else by_channel(term)
+
+        def neighbour(g, ch):
+            cols = slice(ch * CH, (ch + 1) * CH)
+            return g_w[g][:, cols], g_s[:, g * J + ch * CH : g * J + (ch + 1) * CH], w_w, 2, FP4X4, w_s
+
+        def woven(bank):
+            return bank[:].rearrange("p t j -> p j t")
+
+        def copy_out(name, bank, tag=None):
+            res = sb(name, [P, PACK, P], F32, tag)
+            nc.scalar.activation(res[:], bank[:], ACT.Copy)
+            return res
+
+        def running_max(name, bank, so_far, tag=None):
+            larger = sb(name, [P, PACK, P], F32, tag)
+            nc.vector.tensor_tensor(larger[:], bank[:], so_far[:], ALU.max)
+            return larger
+
+        def woven_to(bf, cols):
+            return bf[:, cols.start * PACK : cols.stop * PACK].rearrange("p (a b i) -> p a i b", b=4, i=PACK)
+
+        def woven_from(raw, cols):
+            return raw[:, :, cols].rearrange("p i (a b) -> p a i b", b=4)
 
         def quantize(name, rounded, width):
             words = sb(name + "_w", [P, width], U32)
@@ -65,111 +159,82 @@ def tile_list_pnet_gate_kernel(
             nc.vector.quantize_mx(out=words[:].bitcast(FP8X4), scales=scales[:], in_=rounded[:])
             return words, scales
 
-        w_raw = sb("w_raw", [P, 2 * R], U8)
-        nc.sync.dma_start(out=w_raw[:].bitcast(I32), in_=w_words[0].bitcast(I32))
-        nc.sync.dma_start(out=tab_s[0:P:8, :].bitcast(I32), in_=tab_scales[0].bitcast(I32))
-        load_scale_rows(nc.sync, w_s_raw, w_scales[0])
-        tab_w = sb("tab_w", [P, T], U32)
-        nc.sync.dma_start(out=tab_w[:].bitcast(I32), in_=tab_words[0].rearrange("p t i -> p (t i)").bitcast(I32))
-        picked_s = sb("picked_s", [P, G * J], U8)
-        nc.vector.tensor_copy(picked_s[:], tab_s[:].indirect(offsets[:]))
-        for r in range(4):
-            nc.sync.dma_start(out=g_s[r:P:32, :].bitcast(I32), in_=picked_s[8 * r : P : 32, :].bitcast(I32))
-        wc_raw = sb("wc_raw", [P, PACK, R], F32)
-        nc.sync.dma_start(out=wc_raw[:], in_=wc.rearrange("(p i) r -> p i r", i=PACK))
-        c_raw = [load_c(hf) for hf in range(J // HALF)]
-        wd_w = sb("wd_w", [P, 2 * N], U8)
-        nc.sync.dma_start(out=wd_w[:].bitcast(I32), in_=wd_words[0].bitcast(I32))
-        load_scale_rows(nc.sync, wd_s, wd_scales[0])
-        gate = sb("gate", [P, N // P, J], F32)
-        nc.sync.dma_start(out=gate[:], in_=gm.rearrange("(u p) j -> p u j", p=P))
-
-        w_w = sb("w_w", [P, 2 * R], U8)
-        nc.vector.tensor_copy(
-            w_w[:].bitcast(U16).rearrange("p (t m) -> p t m", t=PACK),
-            w_raw[:].bitcast(U16).rearrange("p (m t) -> p t m", t=PACK),
-        )
-        w_s = sb("w_s", [P, R], U8)
-        nc.vector.tensor_copy(
-            w_s[:].rearrange("p (t m) -> p t m", t=PACK), w_s_raw[:].rearrange("p (m t) -> p t m", t=PACK)
-        )
-
-        g_w = []
-        for g in range(G):
-            g_w.append(sb("g_w%d" % g, [P, J], U32))
-            nc.vector.tensor_copy(g_w[g][:], tab_w[:].indirect(offsets[:, g * J // 16 : (g + 1) * J // 16]))
-
-        def product(psum, *terms):
-            bank = psum.tile([P, PACK, CH], F32, name="bank")
-            for t in range(PACK):
-                for n, (lhs, lhs_elems, lhs_dtype, lhs_s, rhs, rhs_s) in enumerate(terms):
-                    nc.tensor.matmul_mx(
-                        out=bank[:, t, :],
-                        lhsT=lhs[:, t * P * lhs_elems : (t + 1) * P * lhs_elems].bitcast(lhs_dtype),
-                        lhsT_scale=lhs_s[:, t * P : (t + 1) * P],
-                        rhs=rhs.bitcast(FP8X4),
-                        rhs_scale=rhs_s,
-                        start=n == 0,
-                        stop=n == len(terms) - 1,
-                    )
-            return bank
-
-        def neighbour(g, ch):
-            cols = slice(ch * CH, (ch + 1) * CH)
-            return w_w, 2, FP4X4, w_s, g_w[g][:, cols], g_s[:, g * J + ch * CH : g * J + (ch + 1) * CH]
-
-        def woven(bank):
-            return bank[:].rearrange("p t j -> p j t")
-
-        def copy_out(ch, bank):
-            first = sb("first_%d" % ch, [P, CH, PACK], F32)
-            nc.scalar.activation(first[:], woven(bank), ACT.Copy)
-            return first
-
-        firsts = [copy_out(ch, product(psum_a, neighbour(0, ch))) for ch in range(LAST)]
-
-        wc_bf = sb("wc_bf", [P, R * PACK], BF16, "tab_w")
-        wc_to = wc_bf[:].rearrange("p (t m i) -> p m t i", t=PACK, i=PACK)
-        wc_from = wc_raw[:].rearrange("p i (m t) -> p m t i", t=PACK)
-        nc.scalar.activation(wc_to[:, :, :2, :], wc_from[:, :, :2, :], ACT.Copy)
-        nc.gpsimd.tensor_scalar(wc_to[:, :, 2:, :], wc_from[:, :, 2:, :], 1.0, 0.0, ALU.mult, ALU.add)
-        c_bf = []
-        for hf in range(J // HALF):
-            c_bf.append(sb("c_bf%d" % hf, [P, HALF * PACK], BF16))
-            nc.scalar.activation(
-                c_bf[hf][:].rearrange("p (a b i) -> p a i b", b=4, i=PACK),
-                c_raw[hf][:].rearrange("p i (a b) -> p a i b", b=4),
-                ACT.Copy,
+        wc_bf = sb("wc_bf", [P, R * PACK], BF16)
+        for hf, raw in enumerate(wc_raw):
+            nc.gpsimd.tensor_scalar(
+                wc_bf[:].rearrange("p (t m i) -> p m t i", t=PACK, i=PACK)[:, hf * HALF // PACK : (hf + 1) * HALF // PACK],
+                raw[:].rearrange("p i (m t) -> p m t i", t=PACK),
+                1.0,
+                0.0,
+                ALU.mult,
+                ALU.add,
             )
 
-        def running_max(name, bank, so_far, tag=None):
-            larger = sb(name, [P, CH, PACK], F32, tag)
-            nc.vector.tensor_tensor(larger[:], woven(bank), so_far[:], ALU.max)
-            return larger
+        def round_c(hf):
+            rounded = sb("c_bf%d" % hf, [P, HALF * PACK], BF16)
+            nc.scalar.activation(woven_to(rounded, slice(0, HALF)), woven_from(c_raw[hf], slice(0, HALF)), ACT.Copy)
+            return rounded
 
-        pairs = [running_max("pair%d" % ch, product(psum_b, neighbour(1, ch)), firsts[ch]) for ch in range(LAST)]
-        pooled = [running_max("pooled0", product(psum_a, neighbour(2, 0)), pairs[0])]
+        firsts = [copy_out("first%d" % ch, project(ch, neighbour(0, ch))) for ch in range(2)]
+        banks1 = [project(0, neighbour(1, 0))]
+        c_bf = [round_c(0)]
+        banks1.append(project(1, neighbour(1, 1)))
+        firsts.append(copy_out("first2", project(2, neighbour(0, 2)), "c_raw0"))
+        c_bf.append(round_c(1))
+        banks1.append(project(2, neighbour(1, 2)))
+        banks2 = [project(ch, neighbour(2, ch)) for ch in range(LAST)]
+
+        pairs = [running_max("pair%d" % ch, banks1[ch], firsts[ch]) for ch in range(2)]
         wc_w, wc_s = quantize("wc", wc_bf, R)
         c_q = [quantize("c0", c_bf[0], HALF)]
-        pooled.append(running_max("pooled1", product(psum_a, neighbour(2, 1)), pairs[1], "c_bf0"))
+        pairs.append(running_max("pair2", banks1[2], firsts[2]))
+        pooled = [running_max("pooled0", banks2[0], pairs[0], "c_bf0")]
         c_q.append(quantize("c1", c_bf[1], HALF))
-        pooled.append(running_max("pooled2", product(psum_a, neighbour(2, 2)), pairs[2], "c_bf1"))
+        pooled.append(running_max("pooled1", banks2[1], pairs[1], "c_bf1"))
+        pooled.append(running_max("pooled2", banks2[2], pairs[2], "pair1"))
 
         def own(ch):
             hf, cols = ch * CH // HALF, slice(ch * CH % HALF, ch * CH % HALF + CH)
-            return wc_w, 1, FP8X4, wc_s, c_q[hf][0][:, cols], c_q[hf][1][:, cols]
+            return c_q[hf][0][:, cols], c_q[hf][1][:, cols], wc_w, 1, FP8X4, wc_s
 
-        def hidden(ch):
-            bank = product(psum_b, own(ch))
-            z = sb("z%d" % ch, [P, CH, PACK], F32)
-            nc.vector.tensor_tensor(z[:], woven(bank), pooled[ch][:], ALU.add)
+        def turn(bank, part, opens):
+            for t in range(PACK):
+                nc.tensor.matmul(
+                    bank[:, t, :],
+                    part[:, t, :],
+                    ident[:],
+                    is_transpose=True,
+                    start=opens and t == 0,
+                    stop=not opens and t == PACK - 1,
+                )
+
+        def turn_pooled(ch):
+            bank = psum.tile([P, PACK, CH], F32, name="bank")
+            turn(bank, pooled[ch], True)
+            return bank
+
+        def hidden(ch, bank, own_part):
+            turn(bank, own_part, False)
             h_bf = sb("h_bf%d" % ch, [P, CH * PACK], BF16)
-            nc.scalar.activation(h_bf[:], z[:].rearrange("p j t -> p (j t)"), ACT.Relu)
+            nc.scalar.activation(
+                h_bf[:].rearrange("p (j t) -> p j t", t=PACK), bank[:].rearrange("p t j -> p j t"), ACT.Relu
+            )
             return h_bf
 
         def second(ch, h_bf):
             h_w, h_s = quantize("h%d" % ch, h_bf, CH)
-            return product(psum_a, (wd_w, 2, FP4X4, wd_s, h_w[:], h_s[:]))
+            bank = psum.tile([P, PACK, CH], F32, name="bank")
+            for u in range(N // P):
+                nc.tensor.matmul_mx(
+                    out=bank[:, u, :],
+                    lhsT=wd_w[:, 2 * u * P : 2 * (u + 1) * P].bitcast(FP4X4),
+                    lhsT_scale=wd_s[:, u * P : (u + 1) * P],
+                    rhs=h_w[:].bitcast(FP8X4),
+                    rhs_scale=h_s[:],
+                    start=True,
+                    stop=True,
+                )
+            return bank
 
         def finish(ch, bank):
             cols = slice(ch * CH, (ch + 1) * CH)
@@ -181,20 +246,29 @@ def tile_list_pnet_gate_kernel(
                 nc.vector.tensor_tensor(res[:], bank[:, part, :], gate[:, part, cols], ALU.mult)
                 nc.sync.dma_start(out=rows[:, part, :], in_=res[:])
 
-        h_bf = [hidden(0), hidden(1)]
-        first = copy_out(LAST, product(psum_b, neighbour(0, LAST), own(LAST)))
+        own_parts = [copy_out("own%d" % ch, project(ch, own(ch))) for ch in range(TURNED)]
+        sums = [turn_pooled(0)]
+        own_bank = project(2, own(2))
+        h_bf = [hidden(0, sums[0], own_parts[0])]
+        first = sb("first_last", [P, CH, PACK], F32)
+        nc.scalar.activation(first[:], woven(by_channel(neighbour(0, LAST), own(LAST))), ACT.Relu)
+        sums.append(turn_pooled(1))
+        h_bf.append(hidden(1, sums[1], own_parts[1]))
+        z = sb("z", [P, PACK, CH], F32)
+        nc.vector.tensor_tensor(z[:], own_bank[:], pooled[2][:], ALU.add)
+        h_bf.append(sb("h_bf2", [P, CH * PACK], BF16))
+        nc.scalar.activation(woven_to(h_bf[2], slice(0, CH)), woven_from(z, slice(0, CH)), ACT.Relu)
+        bank1 = by_channel(neighbour(1, LAST), own(LAST))
         y_banks = [second(0, h_bf[0])]
-        h_bf.append(hidden(2))
-        bank = product(psum_b, neighbour(1, LAST), own(LAST))
+        bank2 = by_channel(neighbour(2, LAST), own(LAST))
         pair = sb("pair_last", [P, CH, PACK], F32)
-        nc.vector.scalar_tensor_tensor(pair[:], woven(bank), 0.0, first[:], ALU.max, ALU.max)
+        nc.vector.tensor_tensor(pair[:], woven(bank1), first[:], ALU.max)
         y_banks.append(second(1, h_bf[1]))
-        finish(0, y_banks[0])
-        bank = product(psum_b, neighbour(2, LAST), own(LAST))
         h_bf.append(sb("h_bf_last", [P, CH * PACK], BF16))
-        nc.vector.tensor_tensor(h_bf[LAST][:].rearrange("p (j t) -> p j t", t=PACK), woven(bank), pair[:], ALU.max)
+        nc.vector.tensor_tensor(h_bf[LAST][:].rearrange("p (j t) -> p j t", t=PACK), woven(bank2), pair[:], ALU.max)
         y_banks.append(second(2, h_bf[2]))
-        finish(1, y_banks[1])
+        finish(0, y_banks[0])
         y_banks.append(second(LAST, h_bf[LAST]))
+        finish(1, y_banks[1])
         finish(2, y_banks[2])
         finish(LAST, y_banks[LAST])

@@ -24,7 +24,7 @@ CH = 128
 NCH = J // CH
 HALF = 256
 LAST = NCH - 1
-TURNED = 2
+TURNED = 1
 
 
 def load_scale_rows(queue, plane, rows, which=range(4)):
@@ -38,7 +38,7 @@ def tile_list_pnet_gate_kernel(
     nc = tc.nc
     with ExitStack() as ctx:
         keep = ctx.enter_context(tc.tile_pool(name="keep", bufs=1))
-        psum = ctx.enter_context(tc.psum_pool(name="psum", bufs=8))
+        psum = ctx.enter_context(tc.psum_pool(name="psum", bufs=1))
 
         def sb(name, shape, dtype, tag=None):
             return keep.tile(shape, dtype, name=name, tag=tag or name, align_bytes=64)
@@ -49,14 +49,16 @@ def tile_list_pnet_gate_kernel(
         tab_s = sb("tab_s", [P, T], U8)
         w_s_raw = sb("w_s_raw", [P, R], U8)
         wd_s = sb("wd_s", [P, N], U8)
-        g_s = sb("g_s", [P, G * J], U8)
+        g_s = [sb("g_s0", [P, J], U8), sb("g_s1", [P, (G - 1) * J], U8)]
         nc.vector.memset(tab_s[:].bitcast(I32), 0)
         nc.gpsimd.memset(w_s_raw[:].bitcast(I32), 0)
-        nc.vector.memset(g_s[:].bitcast(I32), 0)
+        for plane in g_s:
+            nc.vector.memset(plane[:].bitcast(I32), 0)
         nc.vector.memset(wd_s[:].bitcast(I32), 0)
         load_scale_rows(nc.scalar, w_s_raw, w_scales[0], range(1, 4))
         ident = sb("ident", [P, P], F32)
         make_identity(nc, ident[:])
+        load_scale_rows(nc.gpsimd, wd_s, wd_scales[0])
 
         w_raw = sb("w_raw", [P, 2 * R], U8)
         nc.sync.dma_start(out=w_raw[:].bitcast(I32), in_=w_words[0].bitcast(I32))
@@ -72,25 +74,27 @@ def tile_list_pnet_gate_kernel(
             )
             return raw
 
-        wc_raw = [load_half("wc_raw0", wc, 0)]
+        def pick_scales(n, entries):
+            picked = sb("picked_s%d" % n, [P, entries.stop - entries.start], U8)
+            nc.vector.tensor_copy(picked[:], tab_s[:].indirect(offsets[:, entries.start // 16 : entries.stop // 16]))
+            for r in range(4):
+                nc.sync.dma_start(out=g_s[n][r:P:32, :].bitcast(I32), in_=picked[8 * r : P : 32, :].bitcast(I32))
+
         w_w = sb("w_w", [P, 2 * R], U8)
         nc.vector.tensor_copy(
             w_w[:].bitcast(U16).rearrange("p (t m) -> p t m", t=PACK),
             w_raw[:].bitcast(U16).rearrange("p (m t) -> p t m", t=PACK),
         )
-        picked_s = sb("picked_s", [P, G * J], U8)
-        nc.vector.tensor_copy(picked_s[:], tab_s[:].indirect(offsets[:]))
+        pick_scales(0, slice(0, J))
+        wc_raw = [load_half("wc_raw%d" % hf, wc, hf) for hf in range(R // HALF)]
+        pick_scales(1, slice(J, G * J))
         w_s = sb("w_s", [P, R], U8)
         nc.vector.tensor_copy(
             w_s[:].rearrange("p (t m) -> p t m", t=PACK), w_s_raw[:].rearrange("p (m t) -> p t m", t=PACK)
         )
-        for r in range(4):
-            nc.sync.dma_start(out=g_s[r:P:32, :].bitcast(I32), in_=picked_s[8 * r : P : 32, :].bitcast(I32))
-        wc_raw.append(load_half("wc_raw1", wc, 1))
         c_raw = [load_half("c_raw%d" % hf, c, hf) for hf in range(J // HALF)]
         wd_w = sb("wd_w", [P, 2 * N], U8)
         nc.sync.dma_start(out=wd_w[:].bitcast(I32), in_=wd_words[0].bitcast(I32))
-        load_scale_rows(nc.sync, wd_s, wd_scales[0])
         gate = sb("gate", [P, N // P, J], F32)
         nc.sync.dma_start(out=gate[:], in_=gm.rearrange("(u p) j -> p u j", p=P))
 
@@ -99,8 +103,12 @@ def tile_list_pnet_gate_kernel(
             g_w.append(sb("g_w%d" % g, [P, J], U32))
             nc.vector.tensor_copy(g_w[g][:], tab_w[:].indirect(offsets[:, g * J // 16 : (g + 1) * J // 16]))
 
-        def by_point(points, points_s, weight, weight_bytes, weight_dtype, weight_s):
-            bank = psum.tile([P, PACK, P], F32, name="bank")
+        def new_bank(number, shape):
+            return psum.tile(shape, F32, name="bank%d" % number)
+
+        def by_point(term, number):
+            points, points_s, weight, elems, weight_dtype, weight_s = term
+            bank = new_bank(number, [P, PACK, P])
             nc.tensor.matmul_mx(
                 out=bank[:].rearrange("p t m -> p (t m)"),
                 lhsT=points.bitcast(FP8X4),
@@ -112,39 +120,46 @@ def tile_list_pnet_gate_kernel(
             )
             return bank
 
-        def by_channel(*terms):
-            bank = psum.tile([P, PACK, CH], F32, name="bank")
+        def by_channel(term, number=None, bank=None, closes=True):
+            points, points_s, weight, elems, weight_dtype, weight_s = term
+            opens = bank is None
+            if opens:
+                bank = new_bank(number, [P, PACK, CH])
             for t in range(PACK):
-                for n, (points, points_s, weight, elems, weight_dtype, weight_s) in enumerate(terms):
-                    nc.tensor.matmul_mx(
-                        out=bank[:, t, :],
-                        lhsT=weight[:, t * P * elems : (t + 1) * P * elems].bitcast(weight_dtype),
-                        lhsT_scale=weight_s[:, t * P : (t + 1) * P],
-                        rhs=points.bitcast(FP8X4),
-                        rhs_scale=points_s,
-                        start=n == 0,
-                        stop=n == len(terms) - 1,
-                    )
+                nc.tensor.matmul_mx(
+                    out=bank[:, t, :],
+                    lhsT=weight[:, t * P * elems : (t + 1) * P * elems].bitcast(weight_dtype),
+                    lhsT_scale=weight_s[:, t * P : (t + 1) * P],
+                    rhs=points.bitcast(FP8X4),
+                    rhs_scale=points_s,
+                    start=opens and t == 0,
+                    stop=closes and t == PACK - 1,
+                )
             return bank
 
-        def project(ch, term):
-            return by_point(*term) if ch < TURNED else by_channel(term)
+        def project(ch, term, number):
+            return by_point(term, number) if ch < TURNED else by_channel(term, number)
 
         def neighbour(g, ch):
             cols = slice(ch * CH, (ch + 1) * CH)
-            return g_w[g][:, cols], g_s[:, g * J + ch * CH : g * J + (ch + 1) * CH], w_w, 2, FP4X4, w_s
+            plane = g_s[0] if g == 0 else g_s[1][:, (g - 1) * J : g * J]
+            return g_w[g][:, cols], plane[:, cols], w_w, 2, FP4X4, w_s
 
         def woven(bank):
             return bank[:].rearrange("p t j -> p j t")
 
-        def copy_out(name, bank, tag=None):
-            res = sb(name, [P, PACK, P], F32, tag)
-            nc.scalar.activation(res[:], bank[:], ACT.Copy)
+        def fresh(name):
+            return sb(name, [P, PACK, P], F32)[:]
+
+        def spent(raw, half):
+            return raw[:, 2 * half : 2 * half + 2, :].rearrange("p i (a m) -> p (i a) m", m=P)
+
+        def copy_out(res, bank):
+            nc.scalar.activation(res, bank[:], ACT.Copy)
             return res
 
-        def running_max(name, bank, so_far, tag=None):
-            larger = sb(name, [P, PACK, P], F32, tag)
-            nc.vector.tensor_tensor(larger[:], bank[:], so_far[:], ALU.max)
+        def running_max(larger, bank, so_far):
+            nc.vector.tensor_tensor(larger, bank[:], so_far, ALU.max)
             return larger
 
         def woven_to(bf, cols):
@@ -153,8 +168,8 @@ def tile_list_pnet_gate_kernel(
         def woven_from(raw, cols):
             return raw[:, :, cols].rearrange("p i (a b) -> p a i b", b=4)
 
-        def quantize(name, rounded, width):
-            words = sb(name + "_w", [P, width], U32)
+        def quantize(name, rounded, width, tag=None):
+            words = sb(name + "_w", [P, width], U32, tag)
             scales = sb(name + "_s", [P, width], U8)
             nc.vector.quantize_mx(out=words[:].bitcast(FP8X4), scales=scales[:], in_=rounded[:])
             return words, scales
@@ -175,23 +190,25 @@ def tile_list_pnet_gate_kernel(
             nc.scalar.activation(woven_to(rounded, slice(0, HALF)), woven_from(c_raw[hf], slice(0, HALF)), ACT.Copy)
             return rounded
 
-        firsts = [copy_out("first%d" % ch, project(ch, neighbour(0, ch))) for ch in range(2)]
-        banks1 = [project(0, neighbour(1, 0))]
-        c_bf = [round_c(0)]
-        banks1.append(project(1, neighbour(1, 1)))
-        firsts.append(copy_out("first2", project(2, neighbour(0, 2)), "c_raw0"))
-        c_bf.append(round_c(1))
-        banks1.append(project(2, neighbour(1, 2)))
-        banks2 = [project(ch, neighbour(2, ch)) for ch in range(LAST)]
+        firsts = [copy_out(fresh("first%d" % ch), project(ch, neighbour(0, ch), ch)) for ch in range(2)]
+        banks1 = [project(ch, neighbour(1, ch), 2 + ch) for ch in range(2)]
+        c_bf = [round_c(hf) for hf in range(J // HALF)]
+        firsts.append(copy_out(spent(c_raw[1], 0), project(2, neighbour(0, 2), 4)))
+        banks2 = [project(0, neighbour(2, 0), 5)]
+        banks1.append(project(2, neighbour(1, 2), 6))
+        last_banks = [by_channel(neighbour(g, LAST), number, closes=False) for g, number in ((0, 7), (1, 0))]
+        banks2.append(project(1, neighbour(2, 1), 4))
+        banks2.append(project(2, neighbour(2, 2), 3))
 
-        pairs = [running_max("pair%d" % ch, banks1[ch], firsts[ch]) for ch in range(2)]
+        pairs = [running_max(fresh("pair0"), banks1[0], firsts[0])]
         wc_w, wc_s = quantize("wc", wc_bf, R)
         c_q = [quantize("c0", c_bf[0], HALF)]
-        pairs.append(running_max("pair2", banks1[2], firsts[2]))
-        pooled = [running_max("pooled0", banks2[0], pairs[0], "c_bf0")]
+        pairs.append(running_max(spent(c_raw[0], 0), banks1[1], firsts[1]))
         c_q.append(quantize("c1", c_bf[1], HALF))
-        pooled.append(running_max("pooled1", banks2[1], pairs[1], "c_bf1"))
-        pooled.append(running_max("pooled2", banks2[2], pairs[2], "pair1"))
+        pooled = [running_max(spent(c_raw[1], 1), banks2[0], pairs[0])]
+        pairs.append(running_max(fresh("pair2"), banks1[2], firsts[2]))
+        pooled.append(running_max(fresh("pooled1"), banks2[1], pairs[1]))
+        pooled.append(running_max(fresh("pooled2"), banks2[2], pairs[2]))
 
         def own(ch):
             hf, cols = ch * CH // HALF, slice(ch * CH % HALF, ch * CH % HALF + CH)
@@ -208,67 +225,67 @@ def tile_list_pnet_gate_kernel(
                     stop=not opens and t == PACK - 1,
                 )
 
-        def turn_pooled(ch):
-            bank = psum.tile([P, PACK, CH], F32, name="bank")
-            turn(bank, pooled[ch], True)
+        def turn_own(ch, number):
+            bank = new_bank(number, [P, PACK, CH])
+            turn(bank, own_parts[ch], True)
             return bank
 
-        def hidden(ch, bank, own_part):
-            turn(bank, own_part, False)
-            h_bf = sb("h_bf%d" % ch, [P, CH * PACK], BF16)
-            nc.scalar.activation(
-                h_bf[:].rearrange("p (j t) -> p j t", t=PACK), bank[:].rearrange("p t j -> p j t"), ACT.Relu
-            )
-            return h_bf
+        def hidden(ch, bank, h_bf):
+            turn(bank, pooled[ch], False)
+            nc.scalar.activation(h_bf.rearrange("p (j t) -> p j t", t=PACK), woven(bank), ACT.Relu)
 
-        def second(ch, h_bf):
-            h_w, h_s = quantize("h%d" % ch, h_bf, CH)
-            bank = psum.tile([P, PACK, CH], F32, name="bank")
-            for u in range(N // P):
-                nc.tensor.matmul_mx(
-                    out=bank[:, u, :],
-                    lhsT=wd_w[:, 2 * u * P : 2 * (u + 1) * P].bitcast(FP4X4),
-                    lhsT_scale=wd_s[:, u * P : (u + 1) * P],
-                    rhs=h_w[:].bitcast(FP8X4),
-                    rhs_scale=h_s[:],
-                    start=True,
-                    stop=True,
-                )
-            return bank
+        def second(h_w, h_s, numbers):
+            banks = []
+            for pair_of_tiles in range(N // P // 2):
+                banks.append(new_bank(numbers[pair_of_tiles], [P, 2, HALF]))
+                for k in range(2):
+                    u = 2 * pair_of_tiles + k
+                    nc.tensor.matmul_mx(
+                        out=banks[-1][:, k, :],
+                        lhsT=wd_w[:, 2 * u * P : 2 * (u + 1) * P].bitcast(FP4X4),
+                        lhsT_scale=wd_s[:, u * P : (u + 1) * P],
+                        rhs=h_w[:].bitcast(FP8X4),
+                        rhs_scale=h_s[:],
+                        start=True,
+                        stop=True,
+                    )
+            return banks
 
-        def finish(ch, bank):
-            cols = slice(ch * CH, (ch + 1) * CH)
-            rows = out[:, cols].rearrange("(u p) j -> p u j", p=P)
-            pieces = 2 if ch == LAST else 1
+        def finish(hf, n, bank, pieces=1):
+            cols = slice(hf * HALF, (hf + 1) * HALF)
+            tiles = 2 // pieces
             for k in range(pieces):
-                part = slice(k * PACK // pieces, (k + 1) * PACK // pieces)
-                res = sb("res%d_%d" % (ch, k), [P, PACK // pieces, CH], F32)
-                nc.vector.tensor_tensor(res[:], bank[:, part, :], gate[:, part, cols], ALU.mult)
-                nc.sync.dma_start(out=rows[:, part, :], in_=res[:])
+                part = slice(2 * n + k * tiles, 2 * n + (k + 1) * tiles)
+                res = sb("res%d_%d_%d" % (hf, n, k), [P, tiles, HALF], F32)
+                nc.vector.tensor_tensor(res[:], bank[:, k * tiles : (k + 1) * tiles, :], gate[:, part, cols], ALU.mult)
+                nc.sync.dma_start(out=out[:, cols].rearrange("(u p) j -> p u j", p=P)[:, part, :], in_=res[:])
 
-        own_parts = [copy_out("own%d" % ch, project(ch, own(ch))) for ch in range(TURNED)]
-        sums = [turn_pooled(0)]
-        own_bank = project(2, own(2))
-        h_bf = [hidden(0, sums[0], own_parts[0])]
+        def added(ch, h_bf, number):
+            z = sb("z%d" % ch, [P, PACK, CH], F32)
+            nc.vector.tensor_tensor(z[:], project(ch, own(ch), number)[:], pooled[ch], ALU.add)
+            nc.scalar.activation(woven_to(h_bf, slice(0, CH)), woven_from(z, slice(0, CH)), ACT.Relu)
+
+        own_parts = [copy_out(fresh("own0"), project(0, own(0), 1))]
         first = sb("first_last", [P, CH, PACK], F32)
-        nc.scalar.activation(first[:], woven(by_channel(neighbour(0, LAST), own(LAST))), ACT.Relu)
-        sums.append(turn_pooled(1))
-        h_bf.append(hidden(1, sums[1], own_parts[1]))
-        z = sb("z", [P, PACK, CH], F32)
-        nc.vector.tensor_tensor(z[:], own_bank[:], pooled[2][:], ALU.add)
-        h_bf.append(sb("h_bf2", [P, CH * PACK], BF16))
-        nc.scalar.activation(woven_to(h_bf[2], slice(0, CH)), woven_from(z, slice(0, CH)), ACT.Relu)
-        bank1 = by_channel(neighbour(1, LAST), own(LAST))
-        y_banks = [second(0, h_bf[0])]
-        bank2 = by_channel(neighbour(2, LAST), own(LAST))
+        nc.scalar.activation(first[:], woven(by_channel(own(LAST), bank=last_banks[0])), ACT.Relu)
+        h_01 = sb("h_01", [P, HALF * PACK], BF16)
+        hidden(0, turn_own(0, 1), h_01[:, : CH * PACK])
+        added(1, h_01[:, CH * PACK :], 2)
+        h_bf2 = sb("h_bf2", [P, CH * PACK], BF16)
+        added(2, h_bf2, 5)
         pair = sb("pair_last", [P, CH, PACK], F32)
-        nc.vector.tensor_tensor(pair[:], woven(bank1), first[:], ALU.max)
-        y_banks.append(second(1, h_bf[1]))
-        h_bf.append(sb("h_bf_last", [P, CH * PACK], BF16))
-        nc.vector.tensor_tensor(h_bf[LAST][:].rearrange("p (j t) -> p j t", t=PACK), woven(bank2), pair[:], ALU.max)
-        y_banks.append(second(2, h_bf[2]))
-        finish(0, y_banks[0])
-        y_banks.append(second(LAST, h_bf[LAST]))
-        finish(1, y_banks[1])
-        finish(2, y_banks[2])
-        finish(LAST, y_banks[LAST])
+        nc.vector.tensor_tensor(pair[:], woven(by_channel(own(LAST), bank=last_banks[1])), first[:], ALU.max)
+        bank2 = by_channel(own(LAST), bank=by_channel(neighbour(2, LAST), 6, closes=False))
+        y_banks = [second(*quantize("h01", h_01, HALF), (7, 4))]
+        h_bf3 = sb("h_bf3", [P, CH * PACK], BF16)
+        nc.vector.tensor_tensor(h_bf3[:].rearrange("p (j t) -> p j t", t=PACK), woven(bank2), pair[:], ALU.max)
+        h_w = sb("h23_w", [P, HALF], U32)
+        h_s = sb("h23_s", [P, HALF], U8)
+        for n, rounded in enumerate((h_bf2, h_bf3)):
+            cols = slice(n * CH, (n + 1) * CH)
+            nc.vector.quantize_mx(out=h_w[:, cols].bitcast(FP8X4), scales=h_s[:, cols], in_=rounded[:])
+        y_banks.append(second(h_w, h_s, (3, 1)))
+        finish(0, 0, y_banks[0][0])
+        finish(0, 1, y_banks[0][1])
+        finish(1, 0, y_banks[1][0])
+        finish(1, 1, y_banks[1][1], pieces=2)

@@ -1,7 +1,6 @@
 from contextlib import ExitStack
 
 import concourse.mybir as mybir
-from concourse.masks import make_identity
 
 K, R, N, T, J = 512, 512, 512, 4096, 512
 G = 3
@@ -24,7 +23,8 @@ CH = 128
 NCH = J // CH
 HALF = 256
 LAST = NCH - 1
-TURNED = 1
+TURNED = 0
+BANK = 512
 
 
 def load_scale_rows(queue, plane, rows, which=range(4)):
@@ -56,8 +56,6 @@ def tile_list_pnet_gate_kernel(
             nc.vector.memset(plane[:].bitcast(I32), 0)
         nc.vector.memset(wd_s[:].bitcast(I32), 0)
         load_scale_rows(nc.scalar, w_s_raw, w_scales[0], range(1, 4))
-        ident = sb("ident", [P, P], F32)
-        make_identity(nc, ident[:])
         load_scale_rows(nc.gpsimd, wd_s, wd_scales[0])
 
         w_raw = sb("w_raw", [P, 2 * R], U8)
@@ -148,8 +146,8 @@ def tile_list_pnet_gate_kernel(
         def woven(bank):
             return bank[:].rearrange("p t j -> p j t")
 
-        def fresh(name):
-            return sb(name, [P, PACK, P], F32)[:]
+        def fresh(name, tag=None):
+            return sb(name, [P, PACK, P], F32, tag)[:]
 
         def spent(raw, half):
             return raw[:, 2 * half : 2 * half + 2, :].rearrange("p i (a m) -> p (i a) m", m=P)
@@ -196,9 +194,9 @@ def tile_list_pnet_gate_kernel(
         firsts.append(copy_out(spent(c_raw[1], 0), project(2, neighbour(0, 2), 4)))
         banks2 = [project(0, neighbour(2, 0), 5)]
         banks1.append(project(2, neighbour(1, 2), 6))
-        last_banks = [by_channel(neighbour(g, LAST), number, closes=False) for g, number in ((0, 7), (1, 0))]
-        banks2.append(project(1, neighbour(2, 1), 4))
-        banks2.append(project(2, neighbour(2, 2), 3))
+        banks2.append(project(1, neighbour(2, 1), 0))
+        banks2.append(project(2, neighbour(2, 2), 2))
+        last_bank = by_channel(neighbour(0, LAST), 7, closes=False)
 
         pairs = [running_max(fresh("pair0"), banks1[0], firsts[0])]
         wc_w, wc_s = quantize("wc", wc_bf, R)
@@ -207,41 +205,22 @@ def tile_list_pnet_gate_kernel(
         c_q.append(quantize("c1", c_bf[1], HALF))
         pooled = [running_max(spent(c_raw[1], 1), banks2[0], pairs[0])]
         pairs.append(running_max(fresh("pair2"), banks1[2], firsts[2]))
-        pooled.append(running_max(fresh("pooled1"), banks2[1], pairs[1]))
+        pooled.append(running_max(fresh("pooled1", "c_bf1"), banks2[1], pairs[1]))
         pooled.append(running_max(fresh("pooled2"), banks2[2], pairs[2]))
 
         def own(ch):
             hf, cols = ch * CH // HALF, slice(ch * CH % HALF, ch * CH % HALF + CH)
             return c_q[hf][0][:, cols], c_q[hf][1][:, cols], wc_w, 1, FP8X4, wc_s
 
-        def turn(bank, part, opens):
-            for t in range(PACK):
-                nc.tensor.matmul(
-                    bank[:, t, :],
-                    part[:, t, :],
-                    ident[:],
-                    is_transpose=True,
-                    start=opens and t == 0,
-                    stop=not opens and t == PACK - 1,
-                )
-
-        def turn_own(ch, number):
-            bank = new_bank(number, [P, PACK, CH])
-            turn(bank, own_parts[ch], True)
-            return bank
-
-        def hidden(ch, bank, h_bf):
-            turn(bank, pooled[ch], False)
-            nc.scalar.activation(h_bf.rearrange("p (j t) -> p j t", t=PACK), woven(bank), ACT.Relu)
-
-        def second(h_w, h_s, numbers):
+        def second(h_w, h_s, width, numbers):
+            tiles = BANK // width
             banks = []
-            for pair_of_tiles in range(N // P // 2):
-                banks.append(new_bank(numbers[pair_of_tiles], [P, 2, HALF]))
-                for k in range(2):
-                    u = 2 * pair_of_tiles + k
+            for n, number in enumerate(numbers):
+                banks.append(new_bank(number, [P, tiles, width]))
+                for k in range(tiles):
+                    u = n * tiles + k
                     nc.tensor.matmul_mx(
-                        out=banks[-1][:, k, :],
+                        out=banks[n][:, k, :],
                         lhsT=wd_w[:, 2 * u * P : 2 * (u + 1) * P].bitcast(FP4X4),
                         lhsT_scale=wd_s[:, u * P : (u + 1) * P],
                         rhs=h_w[:].bitcast(FP8X4),
@@ -251,41 +230,43 @@ def tile_list_pnet_gate_kernel(
                     )
             return banks
 
-        def finish(hf, n, bank, pieces=1):
-            cols = slice(hf * HALF, (hf + 1) * HALF)
-            tiles = 2 // pieces
+        def finish(start, width, n, bank, pieces=1):
+            cols = slice(start, start + width)
+            tiles = BANK // width // pieces
             for k in range(pieces):
-                part = slice(2 * n + k * tiles, 2 * n + (k + 1) * tiles)
-                res = sb("res%d_%d_%d" % (hf, n, k), [P, tiles, HALF], F32)
+                part = slice((n * pieces + k) * tiles, (n * pieces + k + 1) * tiles)
+                res = sb("res%d_%d_%d" % (start, n, k), [P, tiles, width], F32)
                 nc.vector.tensor_tensor(res[:], bank[:, k * tiles : (k + 1) * tiles, :], gate[:, part, cols], ALU.mult)
                 nc.sync.dma_start(out=out[:, cols].rearrange("(u p) j -> p u j", p=P)[:, part, :], in_=res[:])
 
-        def added(ch, h_bf, number):
+        def added(ch, engine, own_part):
             z = sb("z%d" % ch, [P, PACK, CH], F32)
-            nc.vector.tensor_tensor(z[:], project(ch, own(ch), number)[:], pooled[ch], ALU.add)
+            engine.tensor_tensor(z[:], own_part, pooled[ch], ALU.add)
+            h_bf = sb("h_bf%d" % ch, [P, CH * PACK], BF16)
             nc.scalar.activation(woven_to(h_bf, slice(0, CH)), woven_from(z, slice(0, CH)), ACT.Relu)
+            return h_bf
 
-        own_parts = [copy_out(fresh("own0"), project(0, own(0), 1))]
+        own_parts = [copy_out(fresh("own%d" % ch), project(ch, own(ch), 1 + 2 * ch)) for ch in range(2)]
         first = sb("first_last", [P, CH, PACK], F32)
-        nc.scalar.activation(first[:], woven(by_channel(own(LAST), bank=last_banks[0])), ACT.Relu)
-        h_01 = sb("h_01", [P, HALF * PACK], BF16)
-        hidden(0, turn_own(0, 1), h_01[:, : CH * PACK])
-        added(1, h_01[:, CH * PACK :], 2)
-        h_bf2 = sb("h_bf2", [P, CH * PACK], BF16)
-        added(2, h_bf2, 5)
+        nc.scalar.activation(first[:], woven(by_channel(own(LAST), bank=last_bank)), ACT.Relu)
+        h_bf = {0: added(0, nc.gpsimd, own_parts[0])}
         pair = sb("pair_last", [P, CH, PACK], F32)
-        nc.vector.tensor_tensor(pair[:], woven(by_channel(own(LAST), bank=last_banks[1])), first[:], ALU.max)
-        bank2 = by_channel(own(LAST), bank=by_channel(neighbour(2, LAST), 6, closes=False))
-        y_banks = [second(*quantize("h01", h_01, HALF), (7, 4))]
-        h_bf3 = sb("h_bf3", [P, CH * PACK], BF16)
-        nc.vector.tensor_tensor(h_bf3[:].rearrange("p (j t) -> p j t", t=PACK), woven(bank2), pair[:], ALU.max)
+        bank1 = by_channel(own(LAST), bank=by_channel(neighbour(1, LAST), 4, closes=False))
+        nc.vector.tensor_tensor(pair[:], woven(bank1), first[:], ALU.max)
+        h_bf[2] = added(2, nc.vector, project(2, own(2), 5)[:])
+        h_bf[1] = added(1, nc.gpsimd, own_parts[1])
+        bank2 = by_channel(own(LAST), bank=by_channel(neighbour(2, LAST), 1, closes=False))
+        y_banks = second(*quantize("h0", h_bf[0], CH), CH, (0,))
+        h_bf[LAST] = sb("h_bf3", [P, CH * PACK], BF16)
+        nc.vector.tensor_tensor(h_bf[LAST][:].rearrange("p (j t) -> p j t", t=PACK), woven(bank2), pair[:], ALU.max)
         h_w = sb("h23_w", [P, HALF], U32)
         h_s = sb("h23_s", [P, HALF], U8)
-        for n, rounded in enumerate((h_bf2, h_bf3)):
-            cols = slice(n * CH, (n + 1) * CH)
-            nc.vector.quantize_mx(out=h_w[:, cols].bitcast(FP8X4), scales=h_s[:, cols], in_=rounded[:])
-        y_banks.append(second(h_w, h_s, (3, 1)))
-        finish(0, 0, y_banks[0][0])
-        finish(0, 1, y_banks[0][1])
-        finish(1, 0, y_banks[1][0])
-        finish(1, 1, y_banks[1][1], pieces=2)
+        for ch in (2, LAST):
+            cols = slice(ch * CH - HALF, (ch + 1) * CH - HALF)
+            nc.vector.quantize_mx(out=h_w[:, cols].bitcast(FP8X4), scales=h_s[:, cols], in_=h_bf[ch][:])
+        y_half = second(h_w, h_s, HALF, (2, 3))
+        finish(0, CH, 0, y_banks[0])
+        y_banks.extend(second(*quantize("h1", h_bf[1], CH), CH, (7,)))
+        finish(HALF, HALF, 0, y_half[0])
+        finish(CH, CH, 0, y_banks[1])
+        finish(HALF, HALF, 1, y_half[1], pieces=2)

@@ -24,7 +24,6 @@ NCH = J // CH
 HALF = 256
 LAST = NCH - 1
 TURNED = 0
-BANK = 512
 
 
 def load_scale_rows(queue, plane, rows, which=range(4)):
@@ -66,9 +65,9 @@ def tile_list_pnet_gate_kernel(
         nc.sync.dma_start(out=tab_w[:].bitcast(I32), in_=tab_words[0].rearrange("p t i -> p (t i)").bitcast(I32))
 
         def load_half(name, matrix, hf):
-            raw = sb(name, [P, PACK, HALF], F32)
+            raw = sb(name, [P, PACK + 2, HALF], F32)
             nc.sync.dma_start(
-                out=raw[:], in_=matrix[:, hf * HALF : (hf + 1) * HALF].rearrange("(p i) j -> p i j", i=PACK)
+                out=raw[:, 1 : PACK + 1, :], in_=matrix[:, hf * HALF : (hf + 1) * HALF].rearrange("(p i) j -> p i j", i=PACK)
             )
             return raw
 
@@ -169,104 +168,94 @@ def tile_list_pnet_gate_kernel(
         def quantize(name, rounded, width, tag=None):
             words = sb(name + "_w", [P, width], U32, tag)
             scales = sb(name + "_s", [P, width], U8)
-            nc.vector.quantize_mx(out=words[:].bitcast(FP8X4), scales=scales[:], in_=rounded[:])
+            nc.vector.quantize_mx(out=words[:].bitcast(FP8X4), scales=scales[:], in_=rounded)
             return words, scales
 
         wc_bf = sb("wc_bf", [P, R * PACK], BF16)
         for hf, raw in enumerate(wc_raw):
             nc.gpsimd.tensor_scalar(
                 wc_bf[:].rearrange("p (t m i) -> p m t i", t=PACK, i=PACK)[:, hf * HALF // PACK : (hf + 1) * HALF // PACK],
-                raw[:].rearrange("p i (m t) -> p m t i", t=PACK),
+                raw[:, 1 : PACK + 1, :].rearrange("p i (m t) -> p m t i", t=PACK),
                 1.0,
                 0.0,
                 ALU.mult,
                 ALU.add,
             )
 
-        def round_c(hf):
-            rounded = sb("c_bf%d" % hf, [P, HALF * PACK], BF16)
-            nc.scalar.activation(woven_to(rounded, slice(0, HALF)), woven_from(c_raw[hf], slice(0, HALF)), ACT.Copy)
-            return rounded
+        c_room = sb("c_room", [P, 3 * CH * PACK], BF16)
+        c_bf = [c_room[:, hf * CH * PACK : (hf + 2) * CH * PACK] for hf in range(J // HALF)]
+
+        def round_on_scalar(hf, cols):
+            nc.scalar.activation(woven_to(c_bf[hf], cols), woven_from(c_raw[hf][:, 1 : PACK + 1, :], cols), ACT.Copy)
 
         firsts = [copy_out(fresh("first%d" % ch), project(ch, neighbour(0, ch), ch)) for ch in range(2)]
         banks1 = [project(ch, neighbour(1, ch), 2 + ch) for ch in range(2)]
-        c_bf = [round_c(hf) for hf in range(J // HALF)]
-        firsts.append(copy_out(spent(c_raw[1], 0), project(2, neighbour(0, 2), 4)))
+        round_on_scalar(0, slice(0, HALF))
+        firsts.append(copy_out(spent(c_raw[0], 0), project(2, neighbour(0, 2), 4)))
+        round_on_scalar(1, slice(CH, HALF))
         banks2 = [project(0, neighbour(2, 0), 5)]
-        banks1.append(project(2, neighbour(1, 2), 6))
-        banks2.append(project(1, neighbour(2, 1), 0))
-        banks2.append(project(2, neighbour(2, 2), 2))
-        last_bank = by_channel(neighbour(0, LAST), 7, closes=False)
+        last_bank = by_channel(neighbour(0, LAST), 6, closes=False)
+        banks2.append(project(1, neighbour(2, 1), 7))
 
         pairs = [running_max(fresh("pair0"), banks1[0], firsts[0])]
-        wc_w, wc_s = quantize("wc", wc_bf, R)
+        wc_w, wc_s = quantize("wc", wc_bf[:], R)
         c_q = [quantize("c0", c_bf[0], HALF)]
-        pairs.append(running_max(spent(c_raw[0], 0), banks1[1], firsts[1]))
+        nc.gpsimd.tensor_scalar(
+            c_bf[1][:, : CH * PACK].rearrange("p (j i) -> p j i", i=PACK),
+            c_raw[1][:, 1 : PACK + 1, :CH].rearrange("p i j -> p j i"),
+            1.0,
+            0.0,
+            ALU.mult,
+            ALU.add,
+        )
+        pairs.append(running_max(spent(c_raw[0], 1), banks1[1], firsts[1]))
+        pooled = [running_max(spent(c_raw[0], 2), banks2[0], pairs[0])]
         c_q.append(quantize("c1", c_bf[1], HALF))
-        pooled = [running_max(spent(c_raw[1], 1), banks2[0], pairs[0])]
-        pairs.append(running_max(fresh("pair2"), banks1[2], firsts[2]))
-        pooled.append(running_max(fresh("pooled1", "c_bf1"), banks2[1], pairs[1]))
-        pooled.append(running_max(fresh("pooled2"), banks2[2], pairs[2]))
+        pooled.append(running_max(fresh("pooled1"), banks2[1], pairs[1]))
 
         def own(ch):
             hf, cols = ch * CH // HALF, slice(ch * CH % HALF, ch * CH % HALF + CH)
             return c_q[hf][0][:, cols], c_q[hf][1][:, cols], wc_w, 1, FP8X4, wc_s
 
-        def second(h_w, h_s, width, numbers):
-            tiles = BANK // width
-            banks = []
-            for n, number in enumerate(numbers):
-                banks.append(new_bank(number, [P, tiles, width]))
-                for k in range(tiles):
-                    u = n * tiles + k
-                    nc.tensor.matmul_mx(
-                        out=banks[n][:, k, :],
-                        lhsT=wd_w[:, 2 * u * P : 2 * (u + 1) * P].bitcast(FP4X4),
-                        lhsT_scale=wd_s[:, u * P : (u + 1) * P],
-                        rhs=h_w[:].bitcast(FP8X4),
-                        rhs_scale=h_s[:],
-                        start=True,
-                        stop=True,
-                    )
-            return banks
+        def second(ch, number):
+            h_w, h_s = quantize("h%d" % ch, h_bf[ch][:], CH)
+            return by_channel((h_w[:], h_s[:], wd_w, 2, FP4X4, wd_s), number)
 
-        def finish(start, width, n, bank, pieces=1):
-            cols = slice(start, start + width)
-            tiles = BANK // width // pieces
+        def finish(ch, bank, pieces=1):
+            cols = slice(ch * CH, (ch + 1) * CH)
+            tiles = PACK // pieces
             for k in range(pieces):
-                part = slice((n * pieces + k) * tiles, (n * pieces + k + 1) * tiles)
-                res = sb("res%d_%d_%d" % (start, n, k), [P, tiles, width], F32)
-                nc.vector.tensor_tensor(res[:], bank[:, k * tiles : (k + 1) * tiles, :], gate[:, part, cols], ALU.mult)
+                part = slice(k * tiles, (k + 1) * tiles)
+                res = sb("res%d_%d" % (ch, k), [P, tiles, CH], F32)
+                nc.vector.tensor_tensor(res[:], bank[:, part, :], gate[:, part, cols], ALU.mult)
                 nc.sync.dma_start(out=out[:, cols].rearrange("(u p) j -> p u j", p=P)[:, part, :], in_=res[:])
 
-        def added(ch, engine, own_part):
-            z = sb("z%d" % ch, [P, PACK, CH], F32)
+        def added(ch, engine, own_part, tag=None, z_tag=None):
+            z = sb("z%d" % ch, [P, PACK, CH], F32, z_tag)
             engine.tensor_tensor(z[:], own_part, pooled[ch], ALU.add)
-            h_bf = sb("h_bf%d" % ch, [P, CH * PACK], BF16)
+            h_bf = sb("h_bf%d" % ch, [P, CH * PACK], BF16, tag)
             nc.scalar.activation(woven_to(h_bf, slice(0, CH)), woven_from(z, slice(0, CH)), ACT.Relu)
             return h_bf
 
-        own_parts = [copy_out(fresh("own%d" % ch), project(ch, own(ch), 1 + 2 * ch)) for ch in range(2)]
+        own_parts = [copy_out(fresh("own%d" % ch), project(ch, own(ch), ch)) for ch in range(2)]
+        pairs.append(running_max(fresh("pair2"), project(2, neighbour(1, 2), 3), firsts[2]))
         first = sb("first_last", [P, CH, PACK], F32)
         nc.scalar.activation(first[:], woven(by_channel(own(LAST), bank=last_bank)), ACT.Relu)
-        h_bf = {0: added(0, nc.gpsimd, own_parts[0])}
-        pair = sb("pair_last", [P, CH, PACK], F32)
-        bank1 = by_channel(own(LAST), bank=by_channel(neighbour(1, LAST), 4, closes=False))
-        nc.vector.tensor_tensor(pair[:], woven(bank1), first[:], ALU.max)
-        h_bf[2] = added(2, nc.vector, project(2, own(2), 5)[:])
+        h_bf = {0: added(0, nc.gpsimd, own_parts[0], z_tag="c_room")}
         h_bf[1] = added(1, nc.gpsimd, own_parts[1])
-        bank2 = by_channel(own(LAST), bank=by_channel(neighbour(2, LAST), 1, closes=False))
-        y_banks = second(*quantize("h0", h_bf[0], CH), CH, (0,))
+        pair = sb("pair_last", [P, CH, PACK], F32)
+        bank1 = by_channel(neighbour(1, LAST), bank=by_channel(own(LAST), 2, closes=False))
+        nc.vector.tensor_tensor(pair[:], woven(bank1), first[:], ALU.max)
+        pooled.append(running_max(fresh("pooled2"), project(2, neighbour(2, 2), 4), pairs[2]))
+        bank2 = by_channel(neighbour(2, LAST), bank=by_channel(own(LAST), 5, closes=False))
         h_bf[LAST] = sb("h_bf3", [P, CH * PACK], BF16)
         nc.vector.tensor_tensor(h_bf[LAST][:].rearrange("p (j t) -> p j t", t=PACK), woven(bank2), pair[:], ALU.max)
-        h_w = sb("h23_w", [P, HALF], U32)
-        h_s = sb("h23_s", [P, HALF], U8)
-        for ch in (2, LAST):
-            cols = slice(ch * CH - HALF, (ch + 1) * CH - HALF)
-            nc.vector.quantize_mx(out=h_w[:, cols].bitcast(FP8X4), scales=h_s[:, cols], in_=h_bf[ch][:])
-        y_half = second(h_w, h_s, HALF, (2, 3))
-        finish(0, CH, 0, y_banks[0])
-        y_banks.extend(second(*quantize("h1", h_bf[1], CH), CH, (7,)))
-        finish(HALF, HALF, 0, y_half[0])
-        finish(CH, CH, 0, y_banks[1])
-        finish(HALF, HALF, 1, y_half[1], pieces=2)
+        y_banks = {0: second(0, 7)}
+        h_bf[2] = added(2, nc.vector, project(2, own(2), 0)[:])
+        y_banks[LAST] = second(LAST, 3)
+        y_banks[1] = second(1, 6)
+        finish(0, y_banks[0])
+        y_banks[2] = second(2, 1)
+        finish(LAST, y_banks[LAST])
+        finish(1, y_banks[1])
+        finish(2, y_banks[2], pieces=2)

@@ -195,7 +195,7 @@ def tile_list_pnet_gate_kernel(
         round_on_scalar(1, slice(CH, HALF))
         banks2 = [project(0, neighbour(2, 0), 5)]
         last_bank = by_channel(neighbour(0, LAST), 6, closes=False)
-        banks2.append(project(1, neighbour(2, 1), 7))
+        banks1.append(project(2, neighbour(1, 2), 7))
 
         pairs = [running_max(fresh("pair0"), banks1[0], firsts[0])]
         wc_w, wc_s = quantize("wc", wc_bf[:], R)
@@ -211,7 +211,7 @@ def tile_list_pnet_gate_kernel(
         pairs.append(running_max(spent(c_raw[0], 1), banks1[1], firsts[1]))
         pooled = [running_max(spent(c_raw[0], 2), banks2[0], pairs[0])]
         c_q.append(quantize("c1", c_bf[1], HALF))
-        pooled.append(running_max(fresh("pooled1"), banks2[1], pairs[1]))
+        pairs.append(running_max(fresh("pair2"), banks1[2], firsts[2]))
 
         def own(ch):
             hf, cols = ch * CH // HALF, slice(ch * CH % HALF, ch * CH % HALF + CH)
@@ -238,24 +238,24 @@ def tile_list_pnet_gate_kernel(
             return h_bf
 
         own_parts = [copy_out(fresh("own%d" % ch), project(ch, own(ch), ch)) for ch in range(2)]
-        pairs.append(running_max(fresh("pair2"), project(2, neighbour(1, 2), 3), firsts[2]))
+        pooled.append(running_max(fresh("pooled1"), project(1, neighbour(2, 1), 3), pairs[1]))
         first = sb("first_last", [P, CH, PACK], F32)
         nc.scalar.activation(first[:], woven(by_channel(own(LAST), bank=last_bank)), ACT.Relu)
         h_bf = {0: added(0, nc.gpsimd, own_parts[0], z_tag="c_room")}
         h_bf[1] = added(1, nc.gpsimd, own_parts[1])
+        pooled.append(running_max(fresh("pooled2"), project(2, neighbour(2, 2), 5), pairs[2]))
         pair = sb("pair_last", [P, CH, PACK], F32)
         bank1 = by_channel(neighbour(1, LAST), bank=by_channel(own(LAST), 2, closes=False))
         nc.vector.tensor_tensor(pair[:], woven(bank1), first[:], ALU.max)
-        pooled.append(running_max(fresh("pooled2"), project(2, neighbour(2, 2), 4), pairs[2]))
-        bank2 = by_channel(neighbour(2, LAST), bank=by_channel(own(LAST), 5, closes=False))
+        h_bf[2] = added(2, nc.vector, project(2, own(2), 4)[:])
+        bank2 = by_channel(neighbour(2, LAST), bank=by_channel(own(LAST), 0, closes=False))
+        y_banks = {0: second(0, 7)}
         h_bf[LAST] = sb("h_bf3", [P, CH * PACK], BF16)
         nc.vector.tensor_tensor(h_bf[LAST][:].rearrange("p (j t) -> p j t", t=PACK), woven(bank2), pair[:], ALU.max)
-        y_banks = {0: second(0, 7)}
-        h_bf[2] = added(2, nc.vector, project(2, own(2), 0)[:])
+        y_banks[1] = second(1, 1)
         y_banks[LAST] = second(LAST, 3)
-        y_banks[1] = second(1, 6)
         finish(0, y_banks[0])
-        y_banks[2] = second(2, 1)
-        finish(LAST, y_banks[LAST])
+        y_banks[2] = second(2, 6)
         finish(1, y_banks[1])
+        finish(LAST, y_banks[LAST])
         finish(2, y_banks[2], pieces=2)

@@ -24,6 +24,7 @@ NCH = J // CH
 HALF = 256
 LAST = NCH - 1
 TURNED = 0
+ROW0 = P - 16
 
 
 def load_scale_rows(queue, plane, rows, which=range(4)):
@@ -49,18 +50,18 @@ def tile_list_pnet_gate_kernel(
         w_s_raw = sb("w_s_raw", [P, R], U8)
         wd_s = sb("wd_s", [P, N], U8)
         g_s = [sb("g_s0", [P, J], U8), sb("g_s1", [P, (G - 1) * J], U8)]
-        nc.vector.memset(tab_s[:].bitcast(I32), 0)
+        nc.sync.dma_start(out=tab_s[ROW0:, :].bitcast(I32), in_=tab_scales[0].bitcast(I32))
+        nc.vector.memset(tab_s[:ROW0, :].bitcast(I32), 0)
         nc.gpsimd.memset(w_s_raw[:].bitcast(I32), 0)
         for plane in g_s:
             nc.vector.memset(plane[:].bitcast(I32), 0)
         nc.vector.memset(wd_s[:].bitcast(I32), 0)
-        load_scale_rows(nc.scalar, w_s_raw, w_scales[0], range(1, 4))
+        load_scale_rows(nc.scalar, w_s_raw, w_scales[0], range(2, 4))
         load_scale_rows(nc.gpsimd, wd_s, wd_scales[0])
 
         w_raw = sb("w_raw", [P, 2 * R], U8)
         nc.sync.dma_start(out=w_raw[:].bitcast(I32), in_=w_words[0].bitcast(I32))
-        load_scale_rows(nc.sync, w_s_raw, w_scales[0], range(1))
-        nc.sync.dma_start(out=tab_s[0:P:8, :].bitcast(I32), in_=tab_scales[0].bitcast(I32))
+        load_scale_rows(nc.sync, w_s_raw, w_scales[0], range(2))
         tab_w = sb("tab_w", [P, T], U32)
         nc.sync.dma_start(out=tab_w[:].bitcast(I32), in_=tab_words[0].rearrange("p t i -> p (t i)").bitcast(I32))
 
@@ -75,16 +76,16 @@ def tile_list_pnet_gate_kernel(
             picked = sb("picked_s%d" % n, [P, entries.stop - entries.start], U8)
             nc.vector.tensor_copy(picked[:], tab_s[:].indirect(offsets[:, entries.start // 16 : entries.stop // 16]))
             for r in range(4):
-                nc.sync.dma_start(out=g_s[n][r:P:32, :].bitcast(I32), in_=picked[8 * r : P : 32, :].bitcast(I32))
+                nc.sync.dma_start(out=g_s[n][r:P:32, :].bitcast(I32), in_=picked[ROW0 + r : P : 4, :].bitcast(I32))
 
+        pick_scales(0, slice(0, J))
+        wc_raw = [load_half("wc_raw%d" % hf, wc, hf) for hf in range(R // HALF)]
+        pick_scales(1, slice(J, G * J))
         w_w = sb("w_w", [P, 2 * R], U8)
         nc.vector.tensor_copy(
             w_w[:].bitcast(U16).rearrange("p (t m) -> p t m", t=PACK),
             w_raw[:].bitcast(U16).rearrange("p (m t) -> p t m", t=PACK),
         )
-        pick_scales(0, slice(0, J))
-        wc_raw = [load_half("wc_raw%d" % hf, wc, hf) for hf in range(R // HALF)]
-        pick_scales(1, slice(J, G * J))
         w_s = sb("w_s", [P, R], U8)
         nc.vector.tensor_copy(
             w_s[:].rearrange("p (t m) -> p t m", t=PACK), w_s_raw[:].rearrange("p (m t) -> p t m", t=PACK)

@@ -25,6 +25,7 @@ HALF = 256
 LAST = NCH - 1
 TURNED = 0
 ROW0 = P - 16
+EARLY = J + HALF
 
 
 def load_scale_rows(queue, plane, rows, which=range(4)):
@@ -49,7 +50,7 @@ def tile_list_pnet_gate_kernel(
         tab_s = sb("tab_s", [P, T], U8)
         w_s_raw = sb("w_s_raw", [P, R], U8)
         wd_s = sb("wd_s", [P, N], U8)
-        g_s = [sb("g_s0", [P, J], U8), sb("g_s1", [P, (G - 1) * J], U8)]
+        g_s = [sb("g_s0", [P, EARLY], U8), sb("g_s1", [P, G * J - EARLY], U8)]
         nc.sync.dma_start(out=tab_s[ROW0:, :].bitcast(I32), in_=tab_scales[0].bitcast(I32))
         nc.vector.memset(tab_s[:ROW0, :].bitcast(I32), 0)
         nc.gpsimd.memset(w_s_raw[:].bitcast(I32), 0)
@@ -78,9 +79,9 @@ def tile_list_pnet_gate_kernel(
             for r in range(4):
                 nc.sync.dma_start(out=g_s[n][r:P:32, :].bitcast(I32), in_=picked[ROW0 + r : P : 4, :].bitcast(I32))
 
-        pick_scales(0, slice(0, J))
+        pick_scales(0, slice(0, EARLY))
         wc_raw = [load_half("wc_raw%d" % hf, wc, hf) for hf in range(R // HALF)]
-        pick_scales(1, slice(J, G * J))
+        pick_scales(1, slice(EARLY, G * J))
         w_w = sb("w_w", [P, 2 * R], U8)
         nc.vector.tensor_copy(
             w_w[:].bitcast(U16).rearrange("p (t m) -> p t m", t=PACK),
@@ -140,8 +141,9 @@ def tile_list_pnet_gate_kernel(
 
         def neighbour(g, ch):
             cols = slice(ch * CH, (ch + 1) * CH)
-            plane = g_s[0] if g == 0 else g_s[1][:, (g - 1) * J : g * J]
-            return g_w[g][:, cols], plane[:, cols], w_w, 2, FP4X4, w_s
+            at = g * J + ch * CH
+            plane = g_s[0][:, at : at + CH] if at < EARLY else g_s[1][:, at - EARLY : at - EARLY + CH]
+            return g_w[g][:, cols], plane, w_w, 2, FP4X4, w_s
 
         def woven(bank):
             return bank[:].rearrange("p t j -> p j t")
@@ -195,8 +197,8 @@ def tile_list_pnet_gate_kernel(
         firsts.append(copy_out(spent(c_raw[0], 0), project(2, neighbour(0, 2), 4)))
         round_on_scalar(1, slice(CH, HALF))
         banks2 = [project(0, neighbour(2, 0), 5)]
-        last_bank = by_channel(neighbour(0, LAST), 6, closes=False)
         banks1.append(project(2, neighbour(1, 2), 7))
+        bank22 = project(2, neighbour(2, 2), 6)
 
         pairs = [running_max(fresh("pair0"), banks1[0], firsts[0])]
         wc_w, wc_s = quantize("wc", wc_bf[:], R)
@@ -240,11 +242,12 @@ def tile_list_pnet_gate_kernel(
 
         own_parts = [copy_out(fresh("own%d" % ch), project(ch, own(ch), ch)) for ch in range(2)]
         pooled.append(running_max(fresh("pooled1"), project(1, neighbour(2, 1), 3), pairs[1]))
+        last_bank = by_channel(neighbour(0, LAST), 5, closes=False)
         first = sb("first_last", [P, CH, PACK], F32)
         nc.scalar.activation(first[:], woven(by_channel(own(LAST), bank=last_bank)), ACT.Relu)
         h_bf = {0: added(0, nc.gpsimd, own_parts[0], z_tag="c_room")}
         h_bf[1] = added(1, nc.gpsimd, own_parts[1])
-        pooled.append(running_max(fresh("pooled2"), project(2, neighbour(2, 2), 5), pairs[2]))
+        pooled.append(running_max(fresh("pooled2"), bank22, pairs[2]))
         pair = sb("pair_last", [P, CH, PACK], F32)
         bank1 = by_channel(neighbour(1, LAST), bank=by_channel(own(LAST), 2, closes=False))
         nc.vector.tensor_tensor(pair[:], woven(bank1), first[:], ALU.max)

@@ -58,7 +58,6 @@ def tile_list_pnet_gate_kernel(
             nc.vector.memset(plane[:].bitcast(I32), 0)
         nc.vector.memset(wd_s[:].bitcast(I32), 0)
         load_scale_rows(nc.scalar, w_s_raw, w_scales[0], range(2, 4))
-        load_scale_rows(nc.gpsimd, wd_s, wd_scales[0])
 
         w_raw = sb("w_raw", [P, 2 * R], U8)
         nc.sync.dma_start(out=w_raw[:].bitcast(I32), in_=w_words[0].bitcast(I32))
@@ -96,6 +95,8 @@ def tile_list_pnet_gate_kernel(
         nc.sync.dma_start(out=wd_w[:].bitcast(I32), in_=wd_words[0].bitcast(I32))
         gate = sb("gate", [P, N // P, J], F32)
         nc.sync.dma_start(out=gate[:], in_=gm.rearrange("(u p) j -> p u j", p=P))
+
+        load_scale_rows(nc.sync, wd_s, wd_scales[0])
 
         g_w = []
         for g in range(G):
@@ -220,8 +221,8 @@ def tile_list_pnet_gate_kernel(
             hf, cols = ch * CH // HALF, slice(ch * CH % HALF, ch * CH % HALF + CH)
             return c_q[hf][0][:, cols], c_q[hf][1][:, cols], wc_w, 1, FP8X4, wc_s
 
-        def second(ch, number):
-            h_w, h_s = quantize("h%d" % ch, h_bf[ch][:], CH)
+        def second(ch, number, tag=None):
+            h_w, h_s = quantize("h%d" % ch, h_bf[ch][:], CH, tag)
             return by_channel((h_w[:], h_s[:], wd_w, 2, FP4X4, wd_s), number)
 
         def finish(ch, bank, pieces=1):
@@ -259,7 +260,7 @@ def tile_list_pnet_gate_kernel(
         y_banks[1] = second(1, 1)
         y_banks[LAST] = second(LAST, 3)
         finish(0, y_banks[0])
-        y_banks[2] = second(2, 6)
+        y_banks[2] = second(2, 6, "h0_w")
         finish(1, y_banks[1])
         finish(LAST, y_banks[LAST])
         finish(2, y_banks[2], pieces=2)

@@ -83,11 +83,15 @@ def tile_list_pnet_gate_kernel(
         pick_scales(1, slice(EARLY, G * J))
         w_w = sb("w_w", [P, 2 * R], U8)
         nc.vector.tensor_copy(
-            w_w[:].bitcast(U16).rearrange("p (t m) -> p t m", t=PACK),
-            w_raw[:].bitcast(U16).rearrange("p (m t) -> p t m", t=PACK),
+            w_w[:].bitcast(U16).rearrange("p (t m) -> p t m", t=PACK)[:, : PACK // 2],
+            w_raw[:].bitcast(U16).rearrange("p (m t) -> p t m", t=PACK)[:, : PACK // 2],
+        )
+        nc.gpsimd.tensor_copy(
+            w_w[:].rearrange("p (t m b) -> p t m b", t=PACK, b=2)[:, PACK // 2 :],
+            w_raw[:].rearrange("p (m t b) -> p t m b", t=PACK, b=2)[:, PACK // 2 :],
         )
         w_s = sb("w_s", [P, R], U8)
-        nc.vector.tensor_copy(
+        nc.gpsimd.tensor_copy(
             w_s[:].rearrange("p (t m) -> p t m", t=PACK), w_s_raw[:].rearrange("p (m t) -> p t m", t=PACK)
         )
         c_raw = [load_half("c_raw%d" % hf, c, hf) for hf in range(J // HALF)]

@@ -20,12 +20,11 @@ ACT = mybir.ActivationFunctionType
 P = 128
 PACK = 4
 CH = 128
-NCH = J // CH
 HALF = 256
-LAST = NCH - 1
-TURNED = 0
+LAST = J // CH - 1
 ROW0 = P - 16
 EARLY = J + HALF
+HEAD = 1024
 
 
 def load_scale_rows(queue, plane, rows, which=range(4)):
@@ -52,25 +51,20 @@ def tile_list_pnet_gate_kernel(
         wd_s = sb("wd_s", [P, N], U8)
         g_s = [sb("g_s0", [P, EARLY], U8), sb("g_s1", [P, G * J - EARLY], U8)]
         nc.sync.dma_start(out=tab_s[ROW0:, :].bitcast(I32), in_=tab_scales[0].bitcast(I32))
+        tab_w = sb("tab_w", [P, T], U32)
+        tab_hbm = tab_words[0].rearrange("p t i -> p (t i)").bitcast(I32)
+        nc.sync.dma_start(out=tab_w[:, :HEAD].bitcast(I32), in_=tab_hbm[:, :HEAD])
         nc.vector.memset(tab_s[:ROW0, :].bitcast(I32), 0)
         nc.gpsimd.memset(w_s_raw[:].bitcast(I32), 0)
         for plane in g_s:
             nc.vector.memset(plane[:].bitcast(I32), 0)
         nc.vector.memset(wd_s[:].bitcast(I32), 0)
         load_scale_rows(nc.scalar, w_s_raw, w_scales[0], range(2, 4))
+        load_scale_rows(nc.sync, w_s_raw, w_scales[0], range(2))
 
+        nc.sync.dma_start(out=tab_w[:, HEAD:].bitcast(I32), in_=tab_hbm[:, HEAD:])
         w_raw = sb("w_raw", [P, 2 * R], U8)
         nc.sync.dma_start(out=w_raw[:].bitcast(I32), in_=w_words[0].bitcast(I32))
-        load_scale_rows(nc.sync, w_s_raw, w_scales[0], range(2))
-        tab_w = sb("tab_w", [P, T], U32)
-        nc.sync.dma_start(out=tab_w[:].bitcast(I32), in_=tab_words[0].rearrange("p t i -> p (t i)").bitcast(I32))
-
-        def load_half(name, matrix, hf):
-            raw = sb(name, [P, PACK + 2, HALF], F32)
-            nc.sync.dma_start(
-                out=raw[:, 1 : PACK + 1, :], in_=matrix[:, hf * HALF : (hf + 1) * HALF].rearrange("(p i) j -> p i j", i=PACK)
-            )
-            return raw
 
         def pick_scales(n, entries):
             picked = sb("picked_s%d" % n, [P, entries.stop - entries.start], U8)
@@ -78,57 +72,43 @@ def tile_list_pnet_gate_kernel(
             for r in range(4):
                 nc.sync.dma_start(out=g_s[n][r:P:32, :].bitcast(I32), in_=picked[ROW0 + r : P : 4, :].bitcast(I32))
 
+        def load_half(name, matrix, hf):
+            raw = sb("%s_raw%d" % (name, hf), [P, PACK + 2, HALF], F32)
+            nc.sync.dma_start(
+                out=raw[:, 1 : PACK + 1, :], in_=matrix[:, hf * HALF : (hf + 1) * HALF].rearrange("(p i) j -> p i j", i=PACK)
+            )
+            return raw
+
         pick_scales(0, slice(0, EARLY))
-        wc_raw = [load_half("wc_raw%d" % hf, wc, hf) for hf in range(R // HALF)]
+        wc_raw = [load_half("wc", wc, hf) for hf in range(R // HALF)]
         pick_scales(1, slice(EARLY, G * J))
-        w_w = sb("w_w", [P, 2 * R], U8)
-        nc.vector.tensor_copy(
-            w_w[:].bitcast(U16).rearrange("p (t m) -> p t m", t=PACK)[:, : PACK // 2],
-            w_raw[:].bitcast(U16).rearrange("p (m t) -> p t m", t=PACK)[:, : PACK // 2],
-        )
-        nc.gpsimd.tensor_copy(
-            w_w[:].rearrange("p (t m b) -> p t m b", t=PACK, b=2)[:, PACK // 2 :],
-            w_raw[:].rearrange("p (m t b) -> p t m b", t=PACK, b=2)[:, PACK // 2 :],
-        )
-        w_s = sb("w_s", [P, R], U8)
-        nc.gpsimd.tensor_copy(
-            w_s[:].rearrange("p (t m) -> p t m", t=PACK), w_s_raw[:].rearrange("p (m t) -> p t m", t=PACK)
-        )
-        c_raw = [load_half("c_raw%d" % hf, c, hf) for hf in range(J // HALF)]
+        c_raw = [load_half("c", c, hf) for hf in range(J // HALF)]
         wd_w = sb("wd_w", [P, 2 * N], U8)
         nc.sync.dma_start(out=wd_w[:].bitcast(I32), in_=wd_words[0].bitcast(I32))
         gate = sb("gate", [P, N // P, J], F32)
         nc.sync.dma_start(out=gate[:], in_=gm.rearrange("(u p) j -> p u j", p=P))
-
         load_scale_rows(nc.sync, wd_s, wd_scales[0])
+
+        w_s = sb("w_s", [P, R], U8)
+        nc.gpsimd.tensor_copy(
+            w_s[:].rearrange("p (t m) -> p t m", t=PACK), w_s_raw[:].rearrange("p (m t) -> p t m", t=PACK)
+        )
+        w_w = sb("w_w", [P, 2 * R], U8)
+        nc.scalar.copy(
+            w_w[:].bitcast(U16).rearrange("p (t m) -> p t m", t=PACK),
+            w_raw[:].bitcast(U16).rearrange("p (m t) -> p t m", t=PACK),
+        )
 
         g_w = []
         for g in range(G):
             g_w.append(sb("g_w%d" % g, [P, J], U32))
             nc.vector.tensor_copy(g_w[g][:], tab_w[:].indirect(offsets[:, g * J // 16 : (g + 1) * J // 16]))
 
-        def new_bank(number, shape):
-            return psum.tile(shape, F32, name="bank%d" % number)
-
-        def by_point(term, number):
-            points, points_s, weight, elems, weight_dtype, weight_s = term
-            bank = new_bank(number, [P, PACK, P])
-            nc.tensor.matmul_mx(
-                out=bank[:].rearrange("p t m -> p (t m)"),
-                lhsT=points.bitcast(FP8X4),
-                lhsT_scale=points_s,
-                rhs=weight[:].bitcast(weight_dtype),
-                rhs_scale=weight_s[:],
-                start=True,
-                stop=True,
-            )
-            return bank
-
-        def by_channel(term, number=None, bank=None, closes=True):
+        def product(term, number=None, bank=None, closes=True):
             points, points_s, weight, elems, weight_dtype, weight_s = term
             opens = bank is None
             if opens:
-                bank = new_bank(number, [P, PACK, CH])
+                bank = psum.tile([P, PACK, CH], F32, name="bank%d" % number)
             for t in range(PACK):
                 nc.tensor.matmul_mx(
                     out=bank[:, t, :],
@@ -141,9 +121,6 @@ def tile_list_pnet_gate_kernel(
                 )
             return bank
 
-        def project(ch, term, number):
-            return by_point(term, number) if ch < TURNED else by_channel(term, number)
-
         def neighbour(g, ch):
             cols = slice(ch * CH, (ch + 1) * CH)
             at = g * J + ch * CH
@@ -154,10 +131,10 @@ def tile_list_pnet_gate_kernel(
             return bank[:].rearrange("p t j -> p j t")
 
         def fresh(name, tag=None):
-            return sb(name, [P, PACK, P], F32, tag)[:]
+            return sb(name, [P, PACK, CH], F32, tag)[:]
 
-        def spent(raw, half):
-            return raw[:, 2 * half : 2 * half + 2, :].rearrange("p i (a m) -> p (i a) m", m=P)
+        def spent(raw, third):
+            return raw[:, 2 * third : 2 * third + 2, :].rearrange("p i (a m) -> p (i a) m", m=CH)
 
         def copy_out(res, bank):
             nc.scalar.activation(res, bank[:], ACT.Copy)
@@ -180,9 +157,10 @@ def tile_list_pnet_gate_kernel(
             return words, scales
 
         wc_bf = sb("wc_bf", [P, R * PACK], BF16)
+        wc_to = wc_bf[:].rearrange("p (t m i) -> p m t i", t=PACK, i=PACK)
         for hf, raw in enumerate(wc_raw):
             nc.gpsimd.tensor_scalar(
-                wc_bf[:].rearrange("p (t m i) -> p m t i", t=PACK, i=PACK)[:, hf * HALF // PACK : (hf + 1) * HALF // PACK],
+                wc_to[:, hf * HALF // PACK : (hf + 1) * HALF // PACK],
                 raw[:, 1 : PACK + 1, :].rearrange("p i (m t) -> p m t i", t=PACK),
                 1.0,
                 0.0,
@@ -196,16 +174,16 @@ def tile_list_pnet_gate_kernel(
         def round_on_scalar(hf, cols):
             nc.scalar.activation(woven_to(c_bf[hf], cols), woven_from(c_raw[hf][:, 1 : PACK + 1, :], cols), ACT.Copy)
 
-        firsts = [copy_out(fresh("first%d" % ch), project(ch, neighbour(0, ch), ch)) for ch in range(2)]
-        banks1 = [project(ch, neighbour(1, ch), 2 + ch) for ch in range(2)]
+        firsts = [copy_out(fresh("first%d" % ch), product(neighbour(0, ch), ch)) for ch in range(2)]
+        seconds = [product(neighbour(1, ch), 2 + ch) for ch in range(2)]
         round_on_scalar(0, slice(0, HALF))
-        firsts.append(copy_out(spent(c_raw[0], 0), project(2, neighbour(0, 2), 4)))
+        firsts.append(copy_out(spent(c_raw[0], 0), product(neighbour(0, 2), 4)))
         round_on_scalar(1, slice(CH, HALF))
-        banks2 = [project(0, neighbour(2, 0), 5)]
-        banks1.append(project(2, neighbour(1, 2), 7))
-        bank22 = project(2, neighbour(2, 2), 6)
+        thirds = [product(neighbour(2, 0), 5)]
+        seconds.append(product(neighbour(1, 2), 7))
+        third_2 = product(neighbour(2, 2), 6)
 
-        pairs = [running_max(fresh("pair0"), banks1[0], firsts[0])]
+        pairs = [running_max(fresh("pair0"), seconds[0], firsts[0])]
         wc_w, wc_s = quantize("wc", wc_bf[:], R)
         c_q = [quantize("c0", c_bf[0], HALF)]
         nc.gpsimd.tensor_scalar(
@@ -216,18 +194,34 @@ def tile_list_pnet_gate_kernel(
             ALU.mult,
             ALU.add,
         )
-        pairs.append(running_max(spent(c_raw[0], 1), banks1[1], firsts[1]))
-        pooled = [running_max(spent(c_raw[0], 2), banks2[0], pairs[0])]
+        pairs.append(running_max(spent(c_raw[0], 1), seconds[1], firsts[1]))
+        pooled = [running_max(spent(c_raw[0], 2), thirds[0], pairs[0])]
         c_q.append(quantize("c1", c_bf[1], HALF))
-        pairs.append(running_max(fresh("pair2"), banks1[2], firsts[2]))
+        pairs.append(running_max(fresh("pair2"), seconds[2], firsts[2]))
 
         def own(ch):
             hf, cols = ch * CH // HALF, slice(ch * CH % HALF, ch * CH % HALF + CH)
             return c_q[hf][0][:, cols], c_q[hf][1][:, cols], wc_w, 1, FP8X4, wc_s
 
-        def second(ch, number, tag=None):
+        def with_own(g, number):
+            return product(own(LAST), bank=product(neighbour(g, LAST), number, closes=False))
+
+        def own_first(g, number):
+            return product(neighbour(g, LAST), bank=product(own(LAST), number, closes=False))
+
+        def added(ch, engine, own_part, tag=None):
+            z = sb("z%d" % ch, [P, PACK, CH], F32, tag)
+            engine.tensor_tensor(z[:], own_part, pooled[ch], ALU.add)
+            return z
+
+        def rectified(ch, z):
+            h_bf = sb("h_bf%d" % ch, [P, CH * PACK], BF16)
+            nc.scalar.activation(woven_to(h_bf, slice(0, CH)), woven_from(z, slice(0, CH)), ACT.Relu)
+            return h_bf
+
+        def second_layer(ch, number, tag=None):
             h_w, h_s = quantize("h%d" % ch, h_bf[ch][:], CH, tag)
-            return by_channel((h_w[:], h_s[:], wd_w, 2, FP4X4, wd_s), number)
+            return product((h_w[:], h_s[:], wd_w, 2, FP4X4, wd_s), number)
 
         def finish(ch, bank, pieces=1):
             cols = slice(ch * CH, (ch + 1) * CH)
@@ -238,33 +232,24 @@ def tile_list_pnet_gate_kernel(
                 nc.vector.tensor_tensor(res[:], bank[:, part, :], gate[:, part, cols], ALU.mult)
                 nc.sync.dma_start(out=out[:, cols].rearrange("(u p) j -> p u j", p=P)[:, part, :], in_=res[:])
 
-        def added(ch, engine, own_part, tag=None, z_tag=None):
-            z = sb("z%d" % ch, [P, PACK, CH], F32, z_tag)
-            engine.tensor_tensor(z[:], own_part, pooled[ch], ALU.add)
-            h_bf = sb("h_bf%d" % ch, [P, CH * PACK], BF16, tag)
-            nc.scalar.activation(woven_to(h_bf, slice(0, CH)), woven_from(z, slice(0, CH)), ACT.Relu)
-            return h_bf
-
-        own_parts = [copy_out(fresh("own%d" % ch), project(ch, own(ch), ch)) for ch in range(2)]
-        pooled.append(running_max(fresh("pooled1"), project(1, neighbour(2, 1), 3), pairs[1]))
-        last_bank = by_channel(neighbour(0, LAST), 5, closes=False)
+        own_parts = [copy_out(fresh("own%d" % ch), product(own(ch), ch)) for ch in range(2)]
+        pooled.append(running_max(fresh("pooled1"), product(neighbour(2, 1), 3), pairs[1]))
         first = sb("first_last", [P, CH, PACK], F32)
-        nc.scalar.activation(first[:], woven(by_channel(own(LAST), bank=last_bank)), ACT.Relu)
-        h_bf = {0: added(0, nc.gpsimd, own_parts[0], z_tag="c_room")}
-        h_bf[1] = added(1, nc.gpsimd, own_parts[1])
-        pooled.append(running_max(fresh("pooled2"), bank22, pairs[2]))
+        nc.scalar.activation(first[:], woven(with_own(0, 5)), ACT.Relu)
+        h_bf = {0: rectified(0, added(0, nc.gpsimd, own_parts[0], "c_room"))}
+        h_bf[1] = rectified(1, added(1, nc.gpsimd, own_parts[1]))
+        pooled.append(running_max(fresh("pooled2"), third_2, pairs[2]))
         pair = sb("pair_last", [P, CH, PACK], F32)
-        bank1 = by_channel(neighbour(1, LAST), bank=by_channel(own(LAST), 2, closes=False))
-        nc.vector.tensor_tensor(pair[:], woven(bank1), first[:], ALU.max)
-        h_bf[2] = added(2, nc.vector, project(2, own(2), 4)[:])
-        bank2 = by_channel(neighbour(2, LAST), bank=by_channel(own(LAST), 0, closes=False))
-        y_banks = {0: second(0, 7)}
+        nc.vector.tensor_tensor(pair[:], woven(own_first(1, 2)), first[:], ALU.max)
+        h_bf[2] = rectified(2, added(2, nc.vector, product(own(2), 4)[:]))
+        last_bank = own_first(2, 0)
+        y_banks = {0: second_layer(0, 7)}
         h_bf[LAST] = sb("h_bf3", [P, CH * PACK], BF16)
-        nc.vector.tensor_tensor(h_bf[LAST][:].rearrange("p (j t) -> p j t", t=PACK), woven(bank2), pair[:], ALU.max)
-        y_banks[1] = second(1, 1)
-        y_banks[LAST] = second(LAST, 3)
+        nc.vector.tensor_tensor(h_bf[LAST][:].rearrange("p (j t) -> p j t", t=PACK), woven(last_bank), pair[:], ALU.max)
+        y_banks[1] = second_layer(1, 1)
+        y_banks[LAST] = second_layer(LAST, 3)
         finish(0, y_banks[0])
-        y_banks[2] = second(2, 6, "h0_w")
+        y_banks[2] = second_layer(2, 6, "h0_w")
         finish(1, y_banks[1])
         finish(LAST, y_banks[LAST])
         finish(2, y_banks[2], pieces=2)

@@ -23,7 +23,7 @@ CH = 128
 HALF = 256
 LAST = J // CH - 1
 ROW0 = P - 16
-EARLY = J + HALF
+EARLY = J + CH
 HEAD = 1024
 
 
@@ -70,7 +70,8 @@ def tile_list_pnet_gate_kernel(
             picked = sb("picked_s%d" % n, [P, entries.stop - entries.start], U8)
             nc.vector.tensor_copy(picked[:], tab_s[:].indirect(offsets[:, entries.start // 16 : entries.stop // 16]))
             for r in range(4):
-                nc.sync.dma_start(out=g_s[n][r:P:32, :].bitcast(I32), in_=picked[ROW0 + r : P : 4, :].bitcast(I32))
+                queue = nc.scalar if n == 0 and r >= 2 else nc.sync
+                queue.dma_start(out=g_s[n][r:P:32, :].bitcast(I32), in_=picked[ROW0 + r : P : 4, :].bitcast(I32))
 
         def load_half(name, matrix, hf):
             raw = sb("%s_raw%d" % (name, hf), [P, PACK + 2, HALF], F32)

@@ -22,9 +22,9 @@ PACK = 4
 CH = 128
 HALF = 256
 LAST = J // CH - 1
-ROW0 = P - 16
+ROW0, ROW_STEP = 32, 4
 EARLY = J + CH
-HEAD = 1024
+HEAD = 512
 
 
 def load_scale_rows(queue, plane, rows, which=range(4)):
@@ -50,17 +50,17 @@ def tile_list_pnet_gate_kernel(
         w_s_raw = sb("w_s_raw", [P, R], U8)
         wd_s = sb("wd_s", [P, N], U8)
         g_s = [sb("g_s0", [P, EARLY], U8), sb("g_s1", [P, G * J - EARLY], U8)]
-        nc.sync.dma_start(out=tab_s[ROW0:, :].bitcast(I32), in_=tab_scales[0].bitcast(I32))
         tab_w = sb("tab_w", [P, T], U32)
         tab_hbm = tab_words[0].rearrange("p t i -> p (t i)").bitcast(I32)
         nc.sync.dma_start(out=tab_w[:, :HEAD].bitcast(I32), in_=tab_hbm[:, :HEAD])
-        nc.vector.memset(tab_s[:ROW0, :].bitcast(I32), 0)
-        nc.gpsimd.memset(w_s_raw[:].bitcast(I32), 0)
+        nc.vector.memset(w_s_raw[:].bitcast(I32), 0)
+        nc.vector.memset(tab_s[:].bitcast(I32), 0)
         for plane in g_s:
             nc.vector.memset(plane[:].bitcast(I32), 0)
         nc.vector.memset(wd_s[:].bitcast(I32), 0)
         load_scale_rows(nc.scalar, w_s_raw, w_scales[0], range(2, 4))
         load_scale_rows(nc.sync, w_s_raw, w_scales[0], range(2))
+        nc.sync.dma_start(out=tab_s[ROW0 : ROW0 + 16 * ROW_STEP : ROW_STEP, :].bitcast(I32), in_=tab_scales[0].bitcast(I32))
 
         nc.sync.dma_start(out=tab_w[:, HEAD:].bitcast(I32), in_=tab_hbm[:, HEAD:])
         w_raw = sb("w_raw", [P, 2 * R], U8)
@@ -71,7 +71,7 @@ def tile_list_pnet_gate_kernel(
             nc.vector.tensor_copy(picked[:], tab_s[:].indirect(offsets[:, entries.start // 16 : entries.stop // 16]))
             for r in range(4):
                 queue = nc.scalar if n == 0 and r >= 2 else nc.sync
-                queue.dma_start(out=g_s[n][r:P:32, :].bitcast(I32), in_=picked[ROW0 + r : P : 4, :].bitcast(I32))
+                queue.dma_start(out=g_s[n][r:P:32, :].bitcast(I32), in_=picked[ROW0 + r * ROW_STEP : ROW0 + 16 * ROW_STEP : 4 * ROW_STEP, :].bitcast(I32))
 
         def load_half(name, matrix, hf):
             raw = sb("%s_raw%d" % (name, hf), [P, PACK + 2, HALF], F32)
@@ -224,14 +224,11 @@ def tile_list_pnet_gate_kernel(
             h_w, h_s = quantize("h%d" % ch, h_bf[ch][:], CH, tag)
             return product((h_w[:], h_s[:], wd_w, 2, FP4X4, wd_s), number)
 
-        def finish(ch, bank, pieces=1):
+        def finish(ch, bank):
             cols = slice(ch * CH, (ch + 1) * CH)
-            tiles = PACK // pieces
-            for k in range(pieces):
-                part = slice(k * tiles, (k + 1) * tiles)
-                res = sb("res%d_%d" % (ch, k), [P, tiles, CH], F32)
-                nc.vector.tensor_tensor(res[:], bank[:, part, :], gate[:, part, cols], ALU.mult)
-                nc.sync.dma_start(out=out[:, cols].rearrange("(u p) j -> p u j", p=P)[:, part, :], in_=res[:])
+            res = sb("res%d" % ch, [P, PACK, CH], F32)
+            nc.vector.tensor_tensor(res[:], bank[:], gate[:, :, cols], ALU.mult)
+            nc.sync.dma_start(out=out[:, cols].rearrange("(u p) j -> p u j", p=P), in_=res[:])
 
         own_parts = [copy_out(fresh("own%d" % ch), product(own(ch), ch)) for ch in range(2)]
         pooled.append(running_max(fresh("pooled1"), product(neighbour(2, 1), 3), pairs[1]))
@@ -253,4 +250,4 @@ def tile_list_pnet_gate_kernel(
         y_banks[2] = second_layer(2, 6, "h0_w")
         finish(1, y_banks[1])
         finish(LAST, y_banks[LAST])
-        finish(2, y_banks[2], pieces=2)
+        finish(2, y_banks[2])

@@ -22,7 +22,7 @@ PACK = 4
 CH = 128
 HALF = 256
 LAST = J // CH - 1
-ROW0, ROW_STEP = 32, 4
+ROW0, ROW_STEP = 4, 8
 EARLY = J + CH
 HEAD = 512
 
@@ -60,7 +60,7 @@ def tile_list_pnet_gate_kernel(
         nc.vector.memset(wd_s[:].bitcast(I32), 0)
         load_scale_rows(nc.scalar, w_s_raw, w_scales[0], range(2, 4))
         load_scale_rows(nc.sync, w_s_raw, w_scales[0], range(2))
-        nc.sync.dma_start(out=tab_s[ROW0 : ROW0 + 16 * ROW_STEP : ROW_STEP, :].bitcast(I32), in_=tab_scales[0].bitcast(I32))
+        nc.sync.dma_start(out=tab_s[ROW0:P:ROW_STEP, :].bitcast(I32), in_=tab_scales[0].bitcast(I32))
 
         nc.sync.dma_start(out=tab_w[:, HEAD:].bitcast(I32), in_=tab_hbm[:, HEAD:])
         w_raw = sb("w_raw", [P, 2 * R], U8)
@@ -71,7 +71,7 @@ def tile_list_pnet_gate_kernel(
             nc.vector.tensor_copy(picked[:], tab_s[:].indirect(offsets[:, entries.start // 16 : entries.stop // 16]))
             for r in range(4):
                 queue = nc.scalar if n == 0 and r >= 2 else nc.sync
-                queue.dma_start(out=g_s[n][r:P:32, :].bitcast(I32), in_=picked[ROW0 + r * ROW_STEP : ROW0 + 16 * ROW_STEP : 4 * ROW_STEP, :].bitcast(I32))
+                queue.dma_start(out=g_s[n][r:P:32, :].bitcast(I32), in_=picked[ROW0 + r * ROW_STEP : P : 4 * ROW_STEP, :].bitcast(I32))
 
         def load_half(name, matrix, hf):
             raw = sb("%s_raw%d" % (name, hf), [P, PACK + 2, HALF], F32)

from contextlib import ExitStack

import concourse.mybir as mybir

K, R, N, T, J = 512, 512, 512, 4096, 512
G = 3
FLOPS = 2 * K * R * J * (G + 1) + 2 * R * N * J

F32 = mybir.dt.float32
BF16 = mybir.dt.bfloat16
I32 = mybir.dt.int32
U32 = mybir.dt.uint32
U16 = mybir.dt.uint16
U8 = mybir.dt.uint8
FP8X4 = mybir.dt.float8_e4m3fn_x4
FP4X4 = mybir.dt.float4_e2m1fn_x4
ALU = mybir.AluOpType
ACT = mybir.ActivationFunctionType

P = 128
PACK = 4
CH = 128
HALF = 256
LAST = J // CH - 1
ROW0, ROW_STEP = 4, 8
EARLY = J + CH
HEAD = 512


def load_scale_rows(queue, plane, rows, which=range(4)):
    for r in which:
        queue.dma_start(out=plane[r:P:32, :].bitcast(I32), in_=rows[r:16:4, :].bitcast(I32))


def tile_list_pnet_gate_kernel(
    tc, tab_words, tab_scales, c, w_words, w_scales, wc, wd_words, wd_scales, gm, offs, out
):
    nc = tc.nc
    with ExitStack() as ctx:
        keep = ctx.enter_context(tc.tile_pool(name="keep", bufs=1))
        psum = ctx.enter_context(tc.psum_pool(name="psum", bufs=1))

        def sb(name, shape, dtype, tag=None):
            return keep.tile(shape, dtype, name=name, tag=tag or name, align_bytes=64)

        offsets = keep.tile([P, G * J // 16], U16, name="offsets")
        nc.sync.dma_start(offsets[:], offs)

        tab_s = sb("tab_s", [P, T], U8)
        w_s_raw = sb("w_s_raw", [P, R], U8)
        wd_s = sb("wd_s", [P, N], U8)
        g_s = [sb("g_s0", [P, EARLY], U8), sb("g_s1", [P, G * J - EARLY], U8)]
        tab_w = sb("tab_w", [P, T], U32)
        tab_hbm = tab_words[0].rearrange("p t i -> p (t i)").bitcast(I32)
        nc.sync.dma_start(out=tab_w[:, :HEAD].bitcast(I32), in_=tab_hbm[:, :HEAD])
        nc.vector.memset(w_s_raw[:].bitcast(I32), 0)
        nc.vector.memset(tab_s[:].bitcast(I32), 0)
        for plane in g_s:
            nc.vector.memset(plane[:].bitcast(I32), 0)
        nc.vector.memset(wd_s[:].bitcast(I32), 0)
        load_scale_rows(nc.scalar, w_s_raw, w_scales[0], range(2, 4))
        load_scale_rows(nc.sync, w_s_raw, w_scales[0], range(2))
        nc.sync.dma_start(out=tab_s[ROW0:P:ROW_STEP, :].bitcast(I32), in_=tab_scales[0].bitcast(I32))

        nc.sync.dma_start(out=tab_w[:, HEAD:].bitcast(I32), in_=tab_hbm[:, HEAD:])
        w_raw = sb("w_raw", [P, 2 * R], U8)
        nc.sync.dma_start(out=w_raw[:].bitcast(I32), in_=w_words[0].bitcast(I32))

        def pick_scales(n, entries):
            picked = sb("picked_s%d" % n, [P, entries.stop - entries.start], U8)
            nc.vector.tensor_copy(picked[:], tab_s[:].indirect(offsets[:, entries.start // 16 : entries.stop // 16]))
            for r in range(4):
                queue = nc.scalar if n == 0 and r >= 2 else nc.sync
                queue.dma_start(out=g_s[n][r:P:32, :].bitcast(I32), in_=picked[ROW0 + r * ROW_STEP : P : 4 * ROW_STEP, :].bitcast(I32))

        def load_half(name, matrix, hf):
            raw = sb("%s_raw%d" % (name, hf), [P, PACK + 2, HALF], F32)
            nc.sync.dma_start(
                out=raw[:, 1 : PACK + 1, :], in_=matrix[:, hf * HALF : (hf + 1) * HALF].rearrange("(p i) j -> p i j", i=PACK)
            )
            return raw

        pick_scales(0, slice(0, EARLY))
        wc_raw = [load_half("wc", wc, hf) for hf in range(R // HALF)]
        pick_scales(1, slice(EARLY, G * J))
        c_raw = [load_half("c", c, hf) for hf in range(J // HALF)]
        wd_w = sb("wd_w", [P, 2 * N], U8)
        nc.sync.dma_start(out=wd_w[:].bitcast(I32), in_=wd_words[0].bitcast(I32))
        gate = sb("gate", [P, N // P, J], F32)
        nc.sync.dma_start(out=gate[:], in_=gm.rearrange("(u p) j -> p u j", p=P))
        load_scale_rows(nc.sync, wd_s, wd_scales[0])

        w_s = sb("w_s", [P, R], U8)
        nc.gpsimd.tensor_copy(
            w_s[:].rearrange("p (t m) -> p t m", t=PACK), w_s_raw[:].rearrange("p (m t) -> p t m", t=PACK)
        )
        w_w = sb("w_w", [P, 2 * R], U8)
        nc.scalar.copy(
            w_w[:].bitcast(U16).rearrange("p (t m) -> p t m", t=PACK),
            w_raw[:].bitcast(U16).rearrange("p (m t) -> p t m", t=PACK),
        )

        g_w = []
        for g in range(G):
            g_w.append(sb("g_w%d" % g, [P, J], U32))
            nc.vector.tensor_copy(g_w[g][:], tab_w[:].indirect(offsets[:, g * J // 16 : (g + 1) * J // 16]))

        def product(term, number=None, bank=None, closes=True):
            points, points_s, weight, elems, weight_dtype, weight_s = term
            opens = bank is None
            if opens:
                bank = psum.tile([P, PACK, CH], F32, name="bank%d" % number)
            for t in range(PACK):
                nc.tensor.matmul_mx(
                    out=bank[:, t, :],
                    lhsT=weight[:, t * P * elems : (t + 1) * P * elems].bitcast(weight_dtype),
                    lhsT_scale=weight_s[:, t * P : (t + 1) * P],
                    rhs=points.bitcast(FP8X4),
                    rhs_scale=points_s,
                    start=opens and t == 0,
                    stop=closes and t == PACK - 1,
                )
            return bank

        def neighbour(g, ch):
            cols = slice(ch * CH, (ch + 1) * CH)
            at = g * J + ch * CH
            plane = g_s[0][:, at : at + CH] if at < EARLY else g_s[1][:, at - EARLY : at - EARLY + CH]
            return g_w[g][:, cols], plane, w_w, 2, FP4X4, w_s

        def woven(bank):
            return bank[:].rearrange("p t j -> p j t")

        def fresh(name, tag=None):
            return sb(name, [P, PACK, CH], F32, tag)[:]

        def spent(raw, third):
            return raw[:, 2 * third : 2 * third + 2, :].rearrange("p i (a m) -> p (i a) m", m=CH)

        def copy_out(res, bank):
            nc.scalar.activation(res, bank[:], ACT.Copy)
            return res

        def running_max(larger, bank, so_far):
            nc.vector.tensor_tensor(larger, bank[:], so_far, ALU.max)
            return larger

        def woven_to(bf, cols):
            return bf[:, cols.start * PACK : cols.stop * PACK].rearrange("p (a b i) -> p a i b", b=4, i=PACK)

        def woven_from(raw, cols):
            return raw[:, :, cols].rearrange("p i (a b) -> p a i b", b=4)

        def quantize(name, rounded, width, tag=None):
            words = sb(name + "_w", [P, width], U32, tag)
            scales = sb(name + "_s", [P, width], U8)
            nc.vector.quantize_mx(out=words[:].bitcast(FP8X4), scales=scales[:], in_=rounded)
            return words, scales

        wc_bf = sb("wc_bf", [P, R * PACK], BF16)
        wc_to = wc_bf[:].rearrange("p (t m i) -> p m t i", t=PACK, i=PACK)
        for hf, raw in enumerate(wc_raw):
            nc.gpsimd.tensor_scalar(
                wc_to[:, hf * HALF // PACK : (hf + 1) * HALF // PACK],
                raw[:, 1 : PACK + 1, :].rearrange("p i (m t) -> p m t i", t=PACK),
                1.0,
                0.0,
                ALU.mult,
                ALU.add,
            )

        c_room = sb("c_room", [P, 3 * CH * PACK], BF16)
        c_bf = [c_room[:, hf * CH * PACK : (hf + 2) * CH * PACK] for hf in range(J // HALF)]

        def round_on_scalar(hf, cols):
            nc.scalar.activation(woven_to(c_bf[hf], cols), woven_from(c_raw[hf][:, 1 : PACK + 1, :], cols), ACT.Copy)

        firsts = [copy_out(fresh("first%d" % ch), product(neighbour(0, ch), ch)) for ch in range(2)]
        seconds = [product(neighbour(1, ch), 2 + ch) for ch in range(2)]
        round_on_scalar(0, slice(0, HALF))
        firsts.append(copy_out(spent(c_raw[0], 0), product(neighbour(0, 2), 4)))
        round_on_scalar(1, slice(CH, HALF))
        thirds = [product(neighbour(2, 0), 5)]
        seconds.append(product(neighbour(1, 2), 7))
        third_2 = product(neighbour(2, 2), 6)

        pairs = [running_max(fresh("pair0"), seconds[0], firsts[0])]
        wc_w, wc_s = quantize("wc", wc_bf[:], R)
        c_q = [quantize("c0", c_bf[0], HALF)]
        nc.gpsimd.tensor_scalar(
            c_bf[1][:, : CH * PACK].rearrange("p (j i) -> p j i", i=PACK),
            c_raw[1][:, 1 : PACK + 1, :CH].rearrange("p i j -> p j i"),
            1.0,
            0.0,
            ALU.mult,
            ALU.add,
        )
        pairs.append(running_max(spent(c_raw[0], 1), seconds[1], firsts[1]))
        pooled = [running_max(spent(c_raw[0], 2), thirds[0], pairs[0])]
        c_q.append(quantize("c1", c_bf[1], HALF))
        pairs.append(running_max(fresh("pair2"), seconds[2], firsts[2]))

        def own(ch):
            hf, cols = ch * CH // HALF, slice(ch * CH % HALF, ch * CH % HALF + CH)
            return c_q[hf][0][:, cols], c_q[hf][1][:, cols], wc_w, 1, FP8X4, wc_s

        def with_own(g, number):
            return product(own(LAST), bank=product(neighbour(g, LAST), number, closes=False))

        def own_first(g, number):
            return product(neighbour(g, LAST), bank=product(own(LAST), number, closes=False))

        def added(ch, engine, own_part, tag=None):
            z = sb("z%d" % ch, [P, PACK, CH], F32, tag)
            engine.tensor_tensor(z[:], own_part, pooled[ch], ALU.add)
            return z

        def rectified(ch, z):
            h_bf = sb("h_bf%d" % ch, [P, CH * PACK], BF16)
            nc.scalar.activation(woven_to(h_bf, slice(0, CH)), woven_from(z, slice(0, CH)), ACT.Relu)
            return h_bf

        def second_layer(ch, number, tag=None):
            h_w, h_s = quantize("h%d" % ch, h_bf[ch][:], CH, tag)
            return product((h_w[:], h_s[:], wd_w, 2, FP4X4, wd_s), number)

        def finish(ch, bank):
            cols = slice(ch * CH, (ch + 1) * CH)
            res = sb("res%d" % ch, [P, PACK, CH], F32)
            nc.vector.tensor_tensor(res[:], bank[:], gate[:, :, cols], ALU.mult)
            nc.sync.dma_start(out=out[:, cols].rearrange("(u p) j -> p u j", p=P), in_=res[:])

        own_parts = [copy_out(fresh("own%d" % ch), product(own(ch), ch)) for ch in range(2)]
        pooled.append(running_max(fresh("pooled1"), product(neighbour(2, 1), 3), pairs[1]))
        first = sb("first_last", [P, CH, PACK], F32)
        nc.scalar.activation(first[:], woven(with_own(0, 5)), ACT.Relu)
        h_bf = {0: rectified(0, added(0, nc.gpsimd, own_parts[0], "c_room"))}
        h_bf[1] = rectified(1, added(1, nc.gpsimd, own_parts[1]))
        pooled.append(running_max(fresh("pooled2"), third_2, pairs[2]))
        pair = sb("pair_last", [P, CH, PACK], F32)
        nc.vector.tensor_tensor(pair[:], woven(own_first(1, 2)), first[:], ALU.max)
        h_bf[2] = rectified(2, added(2, nc.vector, product(own(2), 4)[:]))
        last_bank = own_first(2, 0)
        y_banks = {0: second_layer(0, 7)}
        h_bf[LAST] = sb("h_bf3", [P, CH * PACK], BF16)
        nc.vector.tensor_tensor(h_bf[LAST][:].rearrange("p (j t) -> p j t", t=PACK), woven(last_bank), pair[:], ALU.max)
        y_banks[1] = second_layer(1, 1)
        y_banks[LAST] = second_layer(LAST, 3)
        finish(0, y_banks[0])
        y_banks[2] = second_layer(2, 6, "h0_w")
        finish(1, y_banks[1])
        finish(LAST, y_banks[LAST])
        finish(2, y_banks[2])
